import numpy as np, ml_dtypes
CORES = [9,25,41,57]
N = 4
import mx_ref
BF = ml_dtypes.bfloat16
def gentries(a):
    return np.ascontiguousarray(a.reshape(8, 16, -1).transpose(0, 2, 1)).reshape(8, -1)
def gtable(e):
    e = np.asarray(e); return np.ascontiguousarray(e.reshape(8, -1, 16).transpose(0, 2, 1)).reshape(128, -1).astype(np.int32)
def gcols(t, e):
    v = np.concatenate([t.reshape(8, 16, -1, 4), np.zeros((8, 16, 1, 4), BF)], axis=2)
    return np.ascontiguousarray(np.stack([v[g][:, e[g]] for g in range(8)])).reshape(128, -1)
def gpick(z, e):
    return np.concatenate([z[16 * g:16 * g + 16][:, e[g]] for g in range(8)])
def tile(rs):
    return np.stack(rs, axis=2).reshape(128, -1).astype(BF)
def pick(q, e):
    c = np.concatenate([q[0].reshape(128, -1, 4), np.zeros((128, 1, 4), np.uint8)], axis=1); s = np.concatenate([q[1], np.ones((16, 1), np.uint8)], axis=1)
    return (np.ascontiguousarray(c[:, e].reshape(128, -1)), np.ascontiguousarray(s[:, e]))
def join(*qs):
    return (np.concatenate([q[0] for q in qs], axis=1), np.concatenate([q[1] for q in qs], axis=1))
def put(q, e, v):
    c, s = q[0].reshape(128, -1, 4).copy(), q[1].copy(); c[:, e] = v[0].reshape(128, -1, 4); s[:, e] = v[1]
    return (c.reshape(128, -1), s)
def pk(c, s):
    return (np.ascontiguousarray(c), mx_ref.live(s))
def emit(q):
    return q[0], q[1]
def packed(v, rng):
    q = [mx_ref.quantize(np.ascontiguousarray(v[r])) for r in range(N)]
    return np.stack([a for a, b in q]), np.stack([mx_ref.plane(b, rng) for a, b in q])
def values_of_codes():
    e, c = np.zeros((128, 128, 4), np.float32), np.zeros((128, 2, 4), np.uint8)
    e[np.arange(128), np.arange(128), 0] = 1
    c[:127, :, 0] = np.arange(256).reshape(2, 128).T[:127]
    return mx_ref.matmul(mx_ref.quantize(e.reshape(128, 512).astype(BF)), (c.reshape(128, 8), np.full((16, 2), 127, np.uint8))).T.reshape(-1).astype(np.float64)
CODE_VALUE, SCALE_VALUE = values_of_codes(), 2.0 ** (np.arange(256) - 127.0)
def decode(q):
    return (CODE_VALUE[q[0]].reshape(16, 8, -1, 4) * SCALE_VALUE[q[1]][:, None, :, None] + 0.0).reshape(128, -1).astype(np.float32)
def f(rng, *shape):
    return mx_ref.flush((rng.standard_normal(shape, dtype=np.float32) * np.exp2(rng.integers(-2, 3, shape[:-1] + (1,)))).astype(BF))
def wide(rng, *shape, cols=0):
    v = rng.standard_normal(shape, dtype=np.float32) * np.exp2(rng.integers(-12, 13, shape)).astype(np.float32)
    if cols: v *= np.repeat(np.exp2(rng.integers(-cols, cols + 1, shape[:-2] + (1, shape[-1] // 4))) * (rng.random(shape[:-2] + (1, shape[-1] // 4)) > 0.0625), 4, axis=-1).astype(np.float32)
    return mx_ref.flush(v.astype(BF))
C, H = 448, 224
STEP = [1, 2, 3]
G, OWN = np.arange(8)[:, None], np.tile(np.arange(C), (8, 1))
def numbers_of(rng):
    return {"x": np.array(f(rng, N, 128, 4 * C)), "u": np.array(f(rng, N, 128, 512)), "v": np.array(f(rng, N, 128, 512))}
def stored(a, m):
    return {"fl": np.stack([gtable(a[r]) for r in range(N)]), "ml": np.stack([gtable(m[r]) for r in range(N)])}
def pairs(o):
    m = np.zeros(o.shape, np.int64)
    np.put_along_axis(m, o[..., ::2], o[..., 1::2], axis=-1)
    np.put_along_axis(m, o[..., 1::2], o[..., ::2], axis=-1)
    return m
def ring(o):
    a = np.zeros(C, np.int64)
    a[o] = np.roll(o, -1)
    return a
def lists(rng):
    e = np.tile(np.arange(C), (N, 8, 1))
    return rng.permuted(e, axis=2), pairs(rng.permuted(e, axis=2))
def layers(rng, still=[]):
    w = np.array(f(rng, N, 128, 2048)).reshape(N, 8, 16, 4, 8, 16, 4)
    for i in still:
        w[:, :, i] = 0
        w[:, :, :, :, :, i] = 0
    return w
def weights(rng, w):
    c, s = packed(np.ascontiguousarray(w).reshape(N, 128, 2048), rng)
    return {"wc": c, "ws": s}
def parity():
    i = np.arange(N)
    return (i ^ (i >> 1) ^ (i >> 2)) % 2
def setup_inputs(rng):
    return {**numbers_of(rng), **stored(*lists(rng)), **weights(rng, layers(rng))}
def setup_inputs_ties(rng):
    d = numbers_of(rng)
    o = rng.permutation(N)
    k = rng.integers(0, 4, (N, 8, C))
    k[o[1]] += 1
    k[o[2], rng.permutation(8)[:4]] = 1
    a, m = lists(rng)
    g = int(rng.integers(8))
    a[:, g] = np.arange(C)
    m[:, g] = (np.arange(C) + H) % C
    k[o[3], g] = np.arange(C) >= H
    x = d["x"].reshape(N, 8, 16, C, 4)
    x[:, :, 0] = 0
    x[:, :, 0, :, 0] = k.astype(np.float32).astype(BF)
    u = d["u"].reshape(N, 128, 128, 4)
    u[:, :, ::16] = 0
    for r in range(N):
        for h in range(0, 128, 16): u[r, h, h, 0] = 0.0 if r == o[0] else -1.0 if r == o[1] else 1.0
    return {"x": x.reshape(N, 128, 4 * C), "u": u.reshape(N, 128, 512), "v": d["v"], **stored(a, m), **weights(rng, layers(rng, [0]))}
def setup_inputs_near(rng):
    d = numbers_of(rng)
    x = d["x"].astype(np.float32).reshape(N, 8, 16, C, 4)
    x[:, :, 0] = 0
    x[:, :, 8:] = 0
    x[:, :, 15, :, 0] = 2.0 ** -26
    u = d["u"].reshape(N, 128, 128, 4)
    u[:, :, ::16] = 0
    o = rng.permutation(N) % 4
    for r in range(N):
        c = rng.choice([-1.0, 1.0], (8, 1))
        s = rng.integers(0, 16, (8, C))
        digits = ((s[:, :, None] >> np.arange(4)) & 1) * np.exp2(np.arange(4) - 23.0)
        if o[r] < 2:
            x[r, :, 0, :, 0] = c
            x[r, :, 8] = digits
            x[r, :, 11, :, 0] = 2.0 ** -10
        elif o[r] == 2: x[r, :, 8] = digits * rng.choice([-1.0, 1.0], (8, C, 1))
        else:
            x[r, :, 8, :, 0] = np.where(s < 8, 1.25, 0.0) * 2.0 ** -30 * c
            x[r, :, 9, :, 0] = np.where(s < 8, 0.0, 1.125) * 2.0 ** -30 * c
            for g in rng.permutation(8)[:4]:
                e = rng.choice([-1.0, 1.0], C) * 2.0 ** -30
                x[r, g, 8, :, 0] = 1.25 * e
                x[r, g, 9, :, 0] = -1.125 * e
            x[r, :, 13, :, 0] = rng.choice([-1.0, 1.0], (8, C)) * 2.0 ** -30
        at = [0, C - 1, int(rng.integers(C)), int(rng.integers(C))]
        for g, j in zip(rng.permutation(8)[:4], at): x[r, g, 0, j, 0] = 2.0 ** 29 * rng.choice([-1.0, 1.0])
        k = 1.0 if o[r] == 0 else 2.0 ** -30
        for h in range(0, 128, 16):
            u[r, h, h, 0] = k if o[r] < 2 else 1.0
            if o[r] < 2: u[r, h + 11, h, 0] = k
            if o[r] < 3: u[r, h + 8, h] = k
            else:
                u[r, h + 8, h, 0] = k
                u[r, h + 9, h, 0] = 1.125 * k
                u[r, h + 14, h, 0] = k
    w = layers(rng, [0, 8, 9, 10, 11, 12, 13, 14, 15])
    for g in range(8): w[:, g, 13, 0, g, 14, 0] = 2.0 ** -5
    return {"x": x.reshape(N, 128, 4 * C).astype(BF), "u": u.reshape(N, 128, 512), "v": d["v"], **stored(*lists(rng)), **weights(rng, w)}
def setup_inputs_odd(rng):
    d = numbers_of(rng)
    x = (1.0 + (2 * rng.integers(0, 64, (N, 16, 8, C, 4)) + 1) * 2.0 ** -7) * np.exp2(-rng.integers(0, 7, (N, 16, 8, C, 4)).astype(np.float64)) * rng.choice([-1.0, 1.0], (N, 16, 8, C, 4))
    x[:, :, 0, :, 0] = (np.where((parity()[:, None] + np.arange(16)) % 2 == 0, 1.96875, 1.875) * 2.0 ** 8)[:, :, None]
    x[:, :, 1, :, 0] = rng.integers(8, 16, (N, 16, C)) * 2.0 ** -8
    u = d["u"].reshape(N, 16, 8, 128, 4)
    u[:, :, 0, ::16] = 0
    for r in range(N):
        for g in rng.permutation(8)[:2]:
            u[r, :, :, 16 * g] = 0
            u[r, 2 * g + parity()[r], 1, 16 * g, 0] = 1.0
    w = layers(rng, [0, 1, 8, 9])
    for g in range(8):
        for i in (0, 8): w[:, g, i, 0, g, i, 0] = -0.5
    return {"x": x.astype(np.float32).reshape(N, 128, 4 * C).astype(BF), "u": u.reshape(N, 128, 512), "v": d["v"], **stored(*lists(rng)), **weights(rng, w)}
def setup_inputs_ends(rng):
    d = numbers_of(rng)
    r0 = int(rng.integers(N))
    a = rng.permutation(np.array([r0, r0 ^ STEP[0], r0 ^ STEP[1], r0 ^ STEP[0] ^ STEP[1]]))
    z = rng.permutation(np.setdiff1d(np.arange(N), a))
    x = np.where(rng.random((N, 128, C, 4)) < 0.5, -1.0, -0.9375) * 2.0 ** 30
    x[:, 5] *= 2.0 ** -10
    c = rng.choice([-1.0, 1.0], (128, 1, 4))
    for r in z[:2]: x[r] = c * (1.0 + 0.125 * rng.integers(0, 8, (128, C, 4))) * 2.0 ** -30
    for r in z[2:]: x[r] = x[r] * rng.choice([-1.0, 1.0], (1, C, 1))
    size = np.full(N, 2.0 ** 30)
    size[a[2:]] = 2.0 ** -30
    size[z[1::2]] = 2.0 ** -30
    u = d["u"].astype(np.float32).reshape(N, 128, 128, 4)
    w = np.zeros((N, 128, 4, 128, 4), np.float32)
    i = np.arange(128)
    for b in range(4): w[:, i, b, i, b] = 32.0
    w[a[2], 5, 0, 5, 0] = 2.0 ** 8
    w[a[2], 6, 0, 6, 0] = 2.0 ** -8
    k = np.array([[0, 0, 2, 2, 1, 1, 3, 3], [2, 1, 0, 3, 0, 3, 2, 1]])[parity()][:, rng.permutation(8)]
    e, m = lists(rng)
    j = np.arange(C)
    for r in range(N):
        h = rng.permutation(8)
        u[r, :, ::16] = (np.where(h < 2, 0.0, h % 2 * 2.0 - 1.0) * size[r])[None, :, None]
        for g in range(8):
            t = int(rng.integers(4))
            if t: m[r, g] = [C - 1 - j, j ^ 1, (j + H) % C][t - 1]
            e[r, g] = [ring(rng.permutation(C)), j, ring(j), m[r, g]][k[r, g]]
    u[:, 5, ::16] = 0
    v = rng.choice([-1.0, 1.0], (N, 128, 512)) * size[:, None, None]
    return {"x": x.astype(np.float32).reshape(N, 128, 4 * C).astype(BF), "u": u.reshape(N, 128, 512).astype(BF), "v": v.astype(np.float32).astype(BF), **stored(e, m), **weights(rng, w.astype(BF))}
def setup_inputs_spread(rng):
    d = setup_inputs(rng)
    d["x"] = wide(rng, N, 128, 4 * C, cols=6)
    return d
def check_inputs(d):
    b = []
    for k in ("x", "u", "v"):
        a = np.abs(d[k].astype(np.float32))
        if not (np.isfinite(a).all() and ((a == 0) | (a >= 2.0 ** -30) & (a <= 2.0 ** 30)).all()): b.append("a value of " + k)
    none, least, most = [emit(mx_ref.quantize(np.full((128, 16), k, np.float32).astype(BF)))[1][0, 0] for k in (0.0, 2.0 ** -8, 2.0 ** 8)]
    for r in range(N):
        if (np.sort(gentries(d["fl"][r]), axis=1) != OWN).any(): b.append("fl: a group that doesn't name every column once")
        m = gentries(d["ml"][r])
        if ((m < 0) | (m >= C)).any() or (m == OWN).any() or (m[G, m] != OWN).any(): b.append("ml: columns that aren't each other's mates")
        if ((d["wc"][r] == 0x7F) | (d["wc"][r] == 0xFF)).any(): b.append("wc: a code that is no number")
        s = mx_ref.live(d["ws"][r])
        if ((s != none) & ((s < least) | (s > most))).any(): b.append("ws: a scale out of range")
    return b
def leaders(a, s):
    best, w = OWN, a
    for _ in range(C - 1):
        p, o = s[G, w], s[G, best]
        best = np.where((p > o) | (p == o) & (w < best), w, best)
        w = a[G, w]
    return best
def hops(a, best):
    n, w = np.zeros((8, C), np.int64), best
    for _ in range(C - 1):
        go = w != OWN
        n, w = n + go, np.where(go, a[G, w], w)
    return n
def walk(a, at, n):
    for i in range(C - 1): at = np.where(i < n, a[G, at], at)
    return at
def reference(x, u, v, fl, ml, wc, ws):
    qu = [mx_ref.quantize(u[r]) for r in range(N)]
    lay = [pk(wc[r], ws[r]) for r in range(N)]
    cyc, mate = [gentries(fl[r]) for r in range(N)], [gentries(ml[r]) for r in range(N)]
    now = [x[r] for r in range(N)]
    for step in STEP:
        q = [mx_ref.quantize(now[r]) for r in range(N)]
        t = [decode(q[r]).astype(BF) for r in range(N)]
        made, after = [], []
        for r in range(N):
            p = r ^ step
            s = mx_ref.matmul(qu[r], q[r])[::16] + np.float32(0.0)
            lead = leaders(cyc[r], s)
            far = walk(cyc[p], lead, hops(cyc[r], lead))
            mine = s[G, far]
            other = mine[G, mate[r]]
            swap = np.where(OWN < mate[r], mine < other, other < mine)
            new = cyc[r][G, np.where(swap, mate[r], OWN)]
            back = np.argsort(new, axis=1)
            z = mx_ref.quantize(((gcols(t[r], new).astype(np.float32) + gcols(t[p], far).astype(np.float32)) * np.float32(0.5)).astype(BF))
            res = [mx_ref.matmul(pick(lay[r], np.arange(128 * b, 128 * b + 128)), z) * np.float32(0.03125) for b in range(4)]
            made.append(tile([(t[r][:, b::4].astype(np.float32) + gpick(res[b], back)) * np.float32(0.5) for b in range(4)]))
            after.append(new)
        now, cyc = made, after
    y, nl = np.zeros((N, 128, C), np.float32), np.zeros((N, 8, C), np.float32)
    oc, osc = np.zeros((N, 128, 4 * C), np.uint8), np.zeros((N, 16, C), np.uint8)
    for r in range(N):
        q = mx_ref.quantize(now[r])
        y[r] = mx_ref.matmul(mx_ref.quantize(v[r]), q)
        nl[r] = cyc[r]
        oc[r], osc[r] = emit(q)
    return {"y": y, "nl": nl, "oc": oc, "osc": osc}

@@ -1,0 +1,446 @@
+from concourse.bass import DstId, RemoteDMATransfer
+from concourse.mybir import dt, AluOpType, AxisListType, ActivationFunctionType
+
+C = 448
+TW = 28
+STEP = [1, 2, 3]
+F16 = "float16"
+SCRATCH = {}
+
+
+def _decl():
+    f32, bf = "float32", "bfloat16"
+    for n in ["k0", "k0m", "kc", "cpr", "ka", "kb", "kma", "kmb", "lraw", "ln", "cs", "cp", "rst", "sr", "sa", "pm", "cand",
+              "cm", "mu", "w", "sgn", "ck", "lck", "nlr", "ysb"]:
+        SCRATCH[n] = ("sbuf", [128, C], f32)
+    for n in ["ra", "rb", "eq", "lrow", "drow", "plr", "str_", "lenr", "ar", "trow", "sw", "csr", "lnr", "srow", "brow", "lc",
+              "dq", "lt1", "lt2", "fmr", "mr"]:
+        SCRATCH[n] = ("sbuf", [128, C], bf)
+    SCRATCH["ramp"] = ("sbuf", [128, C + 16], bf)
+    SCRATCH["ca"] = ("sbuf", [128, C], F16)
+    SCRATCH["cb"] = ("sbuf", [128, C], F16)
+    SCRATCH["c4"] = ("sbuf", [128, 4 * C], F16)
+    SCRATCH["gr"] = ("sbuf", [128, 4 * C], bf)
+    for b in range(4):
+        for n in ["fh", "ft", "fs"]:
+            SCRATCH[n + str(b)] = ("sbuf", [128, C], bf)
+        SCRATCH["r2" + str(b)] = ("sbuf", [128, C], f32)
+    for n in ["xin", "xt", "zt"]:
+        SCRATCH[n] = ("sbuf", [128, 4 * C], bf)
+    for n in ["uin", "vin"]:
+        SCRATCH[n] = ("sbuf", [128, 512], bf)
+    SCRATCH["et"] = ("sbuf", [128, 2048], bf)
+    for n, w in [("wq", 512), ("qe", 512), ("qu", 128), ("qur", 128), ("qv", 128), ("qz", C)] + [("qx%d" % i, C) for i in range(4)] + [("lq%d" % i, C) for i in range(3)]:
+        SCRATCH[n] = ("sbuf", [128, w], "float8_e4m3fn_x4")
+        SCRATCH[n + "s"] = ("sbuf", [128, w], "uint8")
+    SCRATCH["fl_s"] = ("sbuf", [128, TW], "int32")
+    SCRATCH["ml_s"] = ("sbuf", [128, TW], "int32")
+    SCRATCH["pcol"] = ("sbuf", [128, 2], "int32")
+    SCRATCH["ofi"] = ("sbuf", [128, 8], "int32")
+    SCRATCH["ofu"] = ("sbuf", [128, 8], "uint16")
+    SCRATCH["col"] = ("sbuf", [128, 8], f32)
+    SCRATCH["tf"] = ("sbuf", [128, TW * 40], f32)
+    SCRATCH["ti"] = ("sbuf", [128, TW * 4], "int32")
+    SCRATCH["tu"] = ("sbuf", [128, TW * 24], "uint16")
+    for i in range(3):
+        SCRATCH["sp%d" % i] = ("sbuf", [128, 3 * TW], "uint16")
+        SCRATCH["sl%d" % i] = ("sbuf", [128, TW], "uint16")
+        SCRATCH["lp%d" % i] = ("sbuf", [128, 3 * TW], "uint16")
+        SCRATCH["la%d" % i] = ("sbuf", [128, TW], "uint16")
+    SCRATCH["pa"] = ("psum", [128, 2048], f32)
+    SCRATCH["pb"] = ("psum", [128, 2048], f32)
+
+
+_decl()
+LOADS = ["dfl", "dml", "dx", "du", "dv", "dwc", "dws"]
+SEMAPHORES = ["cv", "cs_", "ct", "cg", "snt", "outs"] + LOADS + ["%s%d" % (n, i) for n in ("aq", "al", "aa") for i in range(3)]
+TF = {n: i for i, n in enumerate(["jt", "f", "m", "mj", "fm", "dfm", "t", "cs", "ln", "st", "pl", "d", "g0", "g1", "g2", "g3", "i0", "ng", "t1", "ii",
+                                  "pi", "u", "inv", "bq", "t2", "tp", "sw", "sg", "si", "lcur"])}
+TU = {n: i for i, n in enumerate(["tab%d" % k for k in range(9)] + ["m", "root", "d", "pl", "end", "l", "tp", "T", "sig", "b"])}
+TI = {"k": 0, "root": 1, "d": 2, "n": 3}
+
+
+def rank_program(g, core, T, topo):
+    rank = T.rank_of(core)
+    if rank is None:
+        return
+    A = AluOpType
+    AF = ActivationFunctionType
+    Q = {"v": g.vector, "s": g.scalar, "t": g.tensor, "g": g, "y": g.sync}
+    CS = {"v": "cv", "s": "cs_", "t": "ct", "g": "cg"}
+    cnt = {n: 0 for n in SEMAPHORES}
+    known = {e: {} for e in Q}
+    clock = {}
+    lastw, readers = {}, {}
+
+    def need(eng, deps):
+        best = {}
+        for s, v in deps:
+            best[s] = max(best.get(s, 0), v)
+        own = CS.get(eng)
+        for s in sorted(best, key=lambda n: (n == own, n)):
+            v = best[s]
+            if known[eng].get(s, 0) >= v:
+                continue
+            Q[eng].wait_ge(T.sem[s], v)
+            for a, b in clock[(s, v)].items():
+                known[eng][a] = max(known[eng].get(a, 0), b)
+
+    def op(eng, fn, reads, writes, sem=None, inc=1):
+        deps = []
+        for k in reads:
+            if k in lastw:
+                deps.append(lastw[k])
+        for k in writes:
+            if k in lastw:
+                deps.append(lastw[k])
+            for d in readers.get(k, []):
+                deps.append(d)
+        need(eng, deps)
+        s = sem or CS[eng]
+        cnt[s] += inc
+        fn().then_inc(T.sem[s], inc)
+        me = (s, cnt[s])
+        clock[me] = dict(known[eng])
+        clock[me][s] = cnt[s]
+        for k in reads:
+            readers.setdefault(k, []).append(me)
+        for k in writes:
+            lastw[k] = me
+            readers[k] = []
+        return me
+
+    def arrive(sem, n, keys):
+        cnt[sem] += n
+        clock[(sem, n)] = {sem: n}
+        for k in keys:
+            lastw[k] = (sem, n)
+            readers[k] = []
+
+    tf = lambda n: T.tf[:, TW * TF[n]:TW * TF[n] + TW]
+    tu = lambda n: T.tu[:, TW * TU[n]:TW * TU[n] + TW]
+    ti = lambda n: T.ti[:, TW * TI[n]:TW * TI[n] + TW]
+    cl = lambda i: T.col[:, i:i + 1]
+    row = lambda n: T[n][:, 0:C]
+
+    def tt(out, wk, a, b, o, rk):
+        op("v", lambda: g.vector.tensor_tensor(out, a, b, o), rk, wk)
+
+    def ts(out, wk, a, s1, s2, o0, o1, rk):
+        if o1 is None:
+            op("v", lambda: g.vector.tensor_scalar(out, a, s1, None, o0), rk, wk)
+        else:
+            op("v", lambda: g.vector.tensor_scalar(out, a, s1, s2, o0, o1), rk, wk)
+
+    def cp(out, wk, a, rk):
+        op("v", lambda: g.vector.tensor_copy(out, a), rk, wk)
+
+    def act(out, wk, a, rk, func=None, **kw):
+        op("s", lambda: g.scalar.activation(out, a, func or AF.Copy, **kw), rk, wk)
+
+    def scan(out, wk, d0, d1, init, o0, o1, rk):
+        op("v", lambda: g.vector.tensor_tensor_scan(out, d0, d1, init, o0, o1), rk, wk)
+
+    def latch(rname, cname="ca", rap=None, cap=None, rk=None, wk=None):
+        scan(cap if cap is not None else row(cname), [wk or cname], rap if rap is not None else row(rname), row("lc"), -1024.0, A.max, A.add, [rk or rname, "lc"])
+
+    def tabs(cname, out, wk, col):
+        ts(out, wk, T[cname][:, 15:C:16], cl(col), None, A.add, None, [cname, "col%d" % col])
+
+    def tabm(cname, out, wk, col):
+        ts(out, wk, T[cname][:, 15:C:16], -1.0, cl(col), A.mult, A.add, [cname, "col%d" % col])
+
+    def load(eng, sem, out, src, key):
+        op(eng, lambda: Q[eng].dma_start(out, src), [], [key], sem=sem, inc=16)
+    load("y", "dfl", T.fl_s[:], T.fl[:], "fl_s")
+    load("s", "dx", T.xin[:], T.x[:], "xin")
+    load("y", "dml", T.ml_s[:], T.ml[:], "ml_s")
+    load("y", "du", T.uin[:], T.u[:], "uin")
+    load("y", "dwc", T.wq[:, 0:512].bitcast(dt.uint8), T.wc[:], "wq")
+    load("y", "dws", T.wqs[:, 0:512], T.ws[:], "wqs")
+    load("y", "dv", T.vin[:], T.v[:], "vin")
+
+    op("g", lambda: g.iota(T.pcol[:, 0:1], [[0, 1]], 0, 1), [], ["pcol"])
+    op("g", lambda: g.iota(row("dq"), [[0, TW], [1, 16]], 0, 0, allow_small_or_imprecise_dtypes=True), [], ["dq"])
+    op("g", lambda: g.iota(T.ramp[:], [[1, C + 16]], -224, 0, allow_small_or_imprecise_dtypes=True), [], ["ramp"])
+    op("g", lambda: g.iota(row("k0"), [[512, C]], 0, 0, allow_small_or_imprecise_dtypes=True), [], ["k0"])
+    op("g", lambda: g.iota(tf("jt"), [[16, TW]], 0, 0, allow_small_or_imprecise_dtypes=True), [], ["tf.jt"])
+    op("g", lambda: g.iota(T.ofi[:], [[16, 8]], 0, 0), [], ["ofi"])
+    op("g", lambda: g.iota(row("cpr"), [[-1, C]], 449, 0, allow_small_or_imprecise_dtypes=True), [], ["cpr"])
+    ts(T.pcol[:, 1:2], ["pc1"], T.pcol[:, 0:1], 15, None, A.bitwise_and, None, ["pcol"])
+    cp(cl(0), ["col0"], T.pcol[:, 1:2], ["pc1"])
+    ts(row("dq"), ["dq"], row("dq"), cl(0), None, A.subtract, None, ["dq", "col0"])
+    ts(row("lt1"), ["lt1"], row("dq"), 0.0, -1024.0, A.is_lt, A.mult, ["dq"])
+    ts(row("lt2"), ["lt2"], row("dq"), 0.0, 512.0, A.is_equal, A.mult, ["dq"])
+    tt(row("lt1"), ["lt1"], row("lt1"), row("lt2"), A.add, ["lt1", "lt2"])
+    ts(row("lt2"), ["lt2"], row("dq"), 15.0, -1024.0, A.is_equal, A.mult, ["dq"])
+    tt(row("lc"), ["lc"], row("lt1"), row("lt2"), A.add, ["lt1", "lt2"])
+    ts(cl(1), ["col1"], cl(0), 0.0, 1024.0, A.is_equal, A.mult, ["col0"])
+    ts(cl(1), ["col1"], cl(1), -512.0, None, A.add, None, ["col1"])
+    ts(cl(2), ["col2"], cl(1), 224.0, None, A.add, None, ["col1"])
+    cp(tu("tab0"), ["tu.tab0"], T.fl_s[:], ["fl_s"])
+    ts(row("k0m"), ["k0m"], row("k0"), -1.0, None, A.add, None, ["k0"])
+
+    rows = ["ra", "rb"]
+    KS, KM = ["ka", "kb"], ["kma", "kmb"]
+
+    def frow():
+        act(row("ra"), ["ra"], T.ramp[:].indirect(tu("tab0")), ["ramp", "tu.tab0"])
+
+    def lev_row(k):
+        a, b = rows[k % 2], rows[(k + 1) % 2]
+        act(row(b), [b], row(a).indirect(tu("tab%d" % k)), [a, "tu.tab%d" % k])
+
+    def lev_key(k):
+        src = "k0" if k == 0 else KS[k % 2]
+        sm = "k0m" if k == 0 else KM[k % 2]
+        dst = KS[(k + 1) % 2]
+        tt(row(dst), [dst], row(src).indirect(tu("tab%d" % k)), row(sm), A.min, [src, sm, "tu.tab%d" % k])
+
+    def lev_tab(k):
+        b = rows[(k + 1) % 2]
+        latch(b, "ca")
+        tabs("ca", tu("tab%d" % (k + 1)), ["tu.tab%d" % (k + 1)], 2)
+
+    def lev_km(k):
+        a = KS[(k + 1) % 2]
+        m = KM[(k + 1) % 2]
+        act(row(m), [m], row(a), [a], func=AF.Copy, bias=-float(2 ** (k + 1)))
+
+    def level(k):
+        if k < 8:
+            lev_row(k)
+        lev_key(k)
+        if k < 8:
+            lev_tab(k)
+            lev_km(k)
+
+    KF = KS[1]
+
+    def send(dst_name, src_name, sem, code=False, w=C):
+        dst = T.cores[rank ^ STEP[cur[0]]]
+        rid, pid = topo.addr(dst)[0:2]
+        m = topo.mask(core, dst)
+        if code:
+            o, i = T[dst_name][:, 0:w].bitcast(dt.uint8), T[src_name][:, 0:w].bitcast(dt.uint8)
+        else:
+            o, i = T[dst_name][:, 0:w], T[src_name][:, 0:w]
+        need("g", [lastw[src_name]])
+        n = len(topo.engines(core, dst))
+        cnt["snt"] += n
+        g.remote_dma(out_ap=o, in_ap=i, remote_sem=T.sem[sem], local_sem=T.sem.snt, pid=pid, routing_id=rid, dma_engine_mask=m)
+        return n
+
+    cur = [0]
+
+    def finish(r):
+        scan(row("ck"), ["ck"], row(KF), row("lck"), -524288.0, A.max, A.add, [KF, "lck"])
+        ts(ti("k"), ["ti.k"], T.ck[:, 15:C:16], cl(3), None, A.add, None, ["ck", "col3"])
+        ts(ti("root"), ["ti.root"], ti("k"), 9, None, A.arith_shift_right, None, ["ti.k"])
+        tt(row("lraw"), ["lraw"], row(KF).indirect(tu("tab0")), row("kc"), A.subtract, [KF, "tu.tab0", "kc"])
+        cp(tu("root"), ["tu.root"], ti("root"), ["ti.root"])
+        act(row("ln"), ["ln"], row("lraw"), ["lraw"], func=AF.Relu)
+        ts(ti("d"), ["ti.d"], ti("k"), 511, None, A.bitwise_and, None, ["ti.k"])
+        cp(tu("d"), ["tu.d"], ti("d"), ["ti.d"])
+        cp(tf("d"), ["tf.d"], ti("d"), ["ti.d"])
+        act(row("lnr"), ["lnr"], row("ln").indirect(tu("root")), ["ln", "tu.root"], func=AF.Copy, bias=-224.0)
+        scan(row("cs"), ["cs"], row("ln"), row("ln"), 0.0, A.add, A.max, ["ln"])
+        ts(row("csr"), ["csr"], row("cs").indirect(tu("root")), -224.0, None, A.add, None, ["cs", "tu.root"])
+        latch("lnr", "ca")
+        latch("csr", "cb")
+        tabs("ca", tf("ln"), ["tf.ln"], 2)
+        tabs("cb", tf("cs"), ["tf.cs"], 2)
+        tt(tf("st"), ["tf.st"], tf("cs"), tf("ln"), A.subtract, ["tf.cs", "tf.ln"])
+        tt(tf("pl"), ["tf.pl"], tf("st"), tf("d"), A.add, ["tf.st", "tf.d"])
+        cp(tu("pl"), ["tu.pl"], tf("pl"), ["tf.pl"])
+        sp = "sp%d" % r
+        op("v", lambda: g.vector.tensor_copy(row("cp").indirect(tu("pl")), row("cpr")), ["cpr", "tu.pl"], ["cp"])
+        cp(T[sp][:, 0:TW], [sp], tf("pl"), ["tf.pl"])
+        cp(T[sp][:, TW:2 * TW], [sp + "b"], tf("st"), ["tf.st"])
+        cp(T[sp][:, 2 * TW:3 * TW], [sp], tf("ln"), ["tf.ln", sp + "b"])
+        ts(tu("end"), ["tu.end"], tf("cs"), -1.0, None, A.add, None, ["tf.cs"])
+        arrive("al%d" % r, send("lp%d" % r, sp, "al%d" % r, w=3 * TW), ["lp%d" % r])
+        latch("cp", "ca")
+        sl = "sl%d" % r
+        tabm("ca", T[sl][:], [sl], 4)
+        arrive("aa%d" % r, send("la%d" % r, sl, "aa%d" % r, w=TW), ["la%d" % r])
+
+    def sendx(r):
+        cur[0] = r
+        n = send("lq%d" % r, "qx%d" % r, "aq%d" % r, code=True)
+        n += send("lq%ds" % r, "qx%ds" % r, "aq%d" % r)
+        arrive("aq%d" % r, n, ["lq%d" % r, "lq%ds" % r])
+
+    def mm(dst, b, st, so, mv):
+        op("t", lambda: g.tensor.matmul_mx(T[dst][:, 512 * b:512 * b + C], T[st][:, so:so + 128], T[st + "s"][:, so:so + 128], T[mv][:, 0:C], T[mv + "s"][:, 0:C], True, True),
+           [st, st + "s", mv, mv + "s"], [dst + str(b)])
+
+    def quant(tile, keys, w, q):
+        op("v", lambda: g.vector.quantize_mx(T[q][:, 0:w], T[q + "s"][:, 0:w], T[tile][:, 0:4 * w]), keys, [q, q + "s"])
+
+    def scores(r):
+        mm("pb", 0, "qur", 0, "qx%d" % r)
+        for b in range(4):
+            mm("pa", b, "qe", 128 * b, "qx%d" % r)
+
+    frow()
+    level(0)
+    op("v", lambda: g.vector.memset(T.et[:], 1.0), [], ["et"])
+    op("g", lambda: g.affine_select(T.et[:], T.et[:], [[-1, 4], [1, 512]], A.is_equal, 0.0, 0, -4), ["et"], ["et"])
+    cp(tu("m"), ["tu.m"], T.ml_s[:], ["ml_s"])
+    cp(tf("f"), ["tf.f"], T.fl_s[:], ["fl_s"])
+    cp(tf("m"), ["tf.m"], T.ml_s[:], ["ml_s"])
+    act(row("fmr"), ["fmr"], row("ra").indirect(tu("m")), ["ra", "tu.m"])
+    act(row("mr"), ["mr"], T.ramp[:].indirect(tu("m")), ["ramp", "tu.m"])
+    ts(cl(3), ["col3"], cl(1), 512.0, 511.0, A.mult, A.add, ["col1"])
+    ts(cl(4), ["col4"], cl(1), -1.0, 449.0, A.mult, A.add, ["col1"])
+    ts(cl(5), ["col5"], cl(1), -1.0, 224.0, A.mult, A.add, ["col1"])
+    level(1)
+    ts(row("lck"), ["lck"], row("lc"), 512.0, None, A.mult, None, ["lc"])
+    level(2)
+    quant("xin", ["xin"], C, "qx0")
+    sendx(0)
+    level(3)
+    quant("uin", ["uin"], 128, "qu")
+    cp(T.ofu[:], ["ofu"], T.ofi[:], ["ofi"])
+    op("v", lambda: g.vector.tensor_copy(T.qur[:, 0:128].bitcast(dt.uint32), T.qu[:, 0:128].bitcast(dt.uint32).indirect(T.ofu[:, 0:8])), ["qu", "ofu"], ["qur"])
+    op("v", lambda: g.vector.tensor_copy(T.qurs[:, 0:128], T.qus[:, 0:128].indirect(T.ofu[:, 0:8])), ["qus", "ofu"], ["qurs"])
+    level(4)
+    quant("et", ["et"], 512, "qe")
+    scores(0)
+    ts(row("kc"), ["kc"], row("k0"), -512.0, None, A.add, None, ["k0"])
+    level(5)
+    latch("fmr", "cb")
+    tabs("cb", tf("fm"), ["tf.fm"], 2)
+    tt(tf("dfm"), ["tf.dfm"], tf("fm"), tf("f"), A.subtract, ["tf.fm", "tf.f"])
+    ts(tf("jt"), ["tf.jt"], tf("jt"), cl(0), None, A.add, None, ["tf.jt", "col0"])
+    tt(tf("mj"), ["tf.mj"], tf("m"), tf("jt"), A.subtract, ["tf.m", "tf.jt"])
+    level(6)
+    tt(row("sgn"), ["sgn"], row("mr"), T.ramp[:, 0:C], A.is_gt, ["mr", "ramp"])
+    ts(row("sgn"), ["sgn"], row("sgn"), 2.0, -1.0, A.mult, A.add, ["sgn"])
+    level(7)
+    act(row("sr"), ["sr"], T.pb[:, 0:C], ["pb0"])
+    level(8)
+    finish(0)
+
+    for r in range(3):
+        cur[0] = r
+        lq, sl, lp, la = "lq%d" % r, "sl%d" % r, "lp%d" % r, "la%d" % r
+        act(row("rst"), ["rst"], row("ln").indirect(T[sl][:]), ["ln", sl], func=AF.Copy, scale=-float(2 ** 90))
+        cp(row("sa"), ["sa"], row("sr").indirect(T[sl][:]), ["sr", sl])
+        scan(row("pm"), ["pm"], row("rst"), row("sa"), 0.0, A.add, A.max, ["rst", "sa"])
+        tt(row("eq"), ["eq"], row("pm").indirect(tu("end")), row("sr"), A.is_equal, ["pm", "tu.end", "sr"])
+        act(row("drow"), ["drow"], T.ramp[:].indirect(tu("d")), ["ramp", "tu.d"])
+        for b in range(4):
+            mm("pb", b, "qe", 128 * b, lq)
+            act(row("fh%d" % b), ["fh%d" % b], T.pa[:, 512 * b:512 * b + C], ["pa%d" % b], func=AF.Copy, scale=0.5)
+        tt(row("cand"), ["cand"], row("eq").indirect(T[sl][:]), row("cp"), A.mult, ["eq", sl, "cp"])
+        scan(row("cm"), ["cm"], row("rst"), row("cand"), 0.0, A.add, A.max, ["rst", "cand"])
+        ts(row("lrow"), ["lrow"], row("cm").indirect(tu("end")), -225.0, None, A.add, None, ["cm", "tu.end"])
+        latch("lrow", "ca")
+        tabm("ca", tu("l"), ["tu.l"], 5)
+        act(row("str_"), ["str_"], T.ramp[:].indirect(T[lp][:, TW:2 * TW]), ["ramp", lp])
+        act(row("lenr"), ["lenr"], T.ramp[:].indirect(T[lp][:, 2 * TW:3 * TW]), ["ramp", lp])
+        act(row("plr"), ["plr"], T.ramp[:].indirect(T[lp][:, 0:TW]), ["ramp", lp])
+        grs = lambda i: T.gr[:, C * i:C * i + C]
+        c4s = lambda i: T.c4[:, C * i:C * i + C]
+        cp(grs(2), ["gr2"], row("str_").indirect(tu("l")), ["str_", "tu.l"])
+        act(grs(1), ["gr1"], row("drow").indirect(tu("l")), ["drow", "tu.l"])
+        act(grs(0), ["gr0"], row("plr").indirect(tu("l")), ["plr", "tu.l"])
+        cp(grs(3), ["gr3"], row("lenr").indirect(tu("l")), ["lenr", "tu.l"])
+        act(row("ar"), ["ar"], T.ramp[:].indirect(T[la][:]), ["ramp", la])
+        for i in (2, 1, 3, 0):
+            latch(None, rap=grs(i), cap=c4s(i), rk="gr%d" % i, wk="c4%d" % i)
+        ts(T.tf[:, TW * TF["g0"]:TW * (TF["g0"] + 4)], ["tf.g"], T.c4[:, 15:4 * C:16], cl(2), None, A.add, None, ["c40", "c41", "c42", "c43", "col2"])
+        for b in range(4):
+            act(row("ft%d" % b), ["ft%d" % b], T.pb[:, 512 * b:512 * b + C], ["pb%d" % b], func=AF.Copy, scale=0.5)
+        op("v", lambda: g.vector.reciprocal(tf("inv"), tf("g3")), ["tf.g"], ["tf.inv"])
+        tt(tf("i0"), ["tf.i0"], tf("g1"), tf("d"), A.subtract, ["tf.g", "tf.d"])
+        ts(tf("ng"), ["tf.ng"], tf("i0"), 0.0, None, A.is_lt, None, ["tf.i0"])
+        tt(tf("pi"), ["tf.pi"], tf("g0"), tf("i0"), A.subtract, ["tf.g", "tf.i0"])
+        tt(tf("t1"), ["tf.t1"], tf("ng"), tf("ln"), A.mult, ["tf.ng", "tf.ln"])
+        tt(tf("pi"), ["tf.pi"], tf("pi"), tf("t1"), A.subtract, ["tf.pi", "tf.t1"])
+        tt(tf("u"), ["tf.u"], tf("pi"), tf("g2"), A.subtract, ["tf.pi", "tf.g"])
+        tt(tf("bq"), ["tf.bq"], tf("u"), tf("inv"), A.mult, ["tf.u", "tf.inv"])
+        ts(ti("n"), ["ti.n"], tf("bq"), -0.4989, None, A.add, None, ["tf.bq"])
+        tt(tf("t2"), ["tf.t2"], ti("n"), tf("g3"), A.mult, ["ti.n", "tf.g"])
+        tt(tf("tp"), ["tf.tp"], tf("pi"), tf("t2"), A.subtract, ["tf.pi", "tf.t2"])
+        cp(tu("tp"), ["tu.tp"], tf("tp"), ["tf.tp"])
+        cp(row("trow"), ["trow"], row("ar").indirect(tu("tp")), ["ar", "tu.tp"])
+        latch("trow", "ca")
+        tabs("ca", tu("T"), ["tu.T"], 2)
+        tt(row("mu"), ["mu"], row("sr").indirect(tu("T")), row("sgn"), A.mult, ["sr", "tu.T", "sgn"])
+        for b in range(4):
+            act(row("fs%d" % b), ["fs%d" % b], row("ft%d" % b).indirect(tu("T")), ["ft%d" % b, "tu.T"])
+            if b == 0:
+                act(row("w"), ["w"], row("mu"), ["mu"], func=AF.Copy, scale=-1.0)
+        tt(row("sw"), ["sw"], row("mu").indirect(tu("m")), row("w"), A.is_lt, ["mu", "w", "tu.m"])
+        latch("sw", "ca")
+        tabs("ca", tf("sw"), ["tf.sw"], 1)
+        tt(tf("t"), ["tf.t"], tf("sw"), tf("dfm"), A.mult, ["tf.sw", "tf.dfm"])
+        tt(tf("f"), ["tf.f"], tf("f"), tf("t"), A.add, ["tf.f", "tf.t"])
+        cp(tu("tab0"), ["tu.tab0"], tf("f"), ["tf.f"])
+        last = r == 2
+        if not last:
+            frow()
+            lev_row(0)
+        else:
+            act(row("nlr"), ["nlr"], T.ramp[:].indirect(tu("tab0")), ["ramp", "tu.tab0"], func=AF.Copy, bias=224.0)
+        for b in range(4):
+            tt(T.zt[:, b:4 * C:4], ["zt%d" % b], row("fh%d" % b).indirect(tu("tab0")), row("fs%d" % b), A.add, ["fh%d" % b, "fs%d" % b, "tu.tab0"])
+            if b == 0 and r > 0:
+                tt(tf("sg"), ["tf.sg"], tf("sw"), tf("mj"), A.mult, ["tf.sw", "tf.mj"])
+            if b == 1 and r > 0:
+                tt(tf("si"), ["tf.si"], tf("sg"), tf("jt"), A.add, ["tf.sg", "tf.jt"])
+            if b == 2 and r > 0:
+                cp(tu("sig"), ["tu.sig"], tf("si"), ["tf.si"])
+        quant("zt", ["zt0", "zt1", "zt2", "zt3"], C, "qz")
+        for b in range(4):
+            mm("pa", b, "wq", 128 * b, "qz")
+        if r == 0:
+            op("v", lambda: g.vector.tensor_copy(row("brow").indirect(tu("tab0")), T.ramp[:, 0:C]), ["ramp", "tu.tab0"], ["brow"])
+        else:
+            act(row("srow"), ["srow"], T.ramp[:].indirect(tu("sig")), ["ramp", "tu.sig"])
+            act(row("brow"), ["brow"], row("srow").indirect(tu("b")), ["srow", "tu.b"])
+        for b in range(4):
+            act(row("r2%d" % b), ["r2%d" % b], T.pa[:, 512 * b:512 * b + C], ["pa%d" % b], func=AF.Copy, scale=0.015625)
+        if not last:
+            ts(tf("t"), ["tf.t"], tf("t"), -2.0, None, A.mult, None, ["tf.t"])
+            lev_key(0)
+            lev_km(0)
+            tt(tf("dfm"), ["tf.dfm"], tf("dfm"), tf("t"), A.add, ["tf.dfm", "tf.t"])
+        latch("brow", "cb")
+        tabs("cb", tu("b"), ["tu.b"], 2)
+        if not last:
+            lev_tab(0)
+        for b in range(4):
+            tt(T.xt[:, b:4 * C:4], ["xt%d" % b], row("r2%d" % b).indirect(tu("b")), row("fh%d" % b), A.add, ["r2%d" % b, "fh%d" % b, "tu.b"])
+        qn = "qx%d" % (r + 1)
+        if not last:
+            lev_row(1)
+        quant("xt", ["xt0", "xt1", "xt2", "xt3"], C, qn)
+        if not last:
+            sendx(r + 1)
+            scores(r + 1)
+            lev_key(1)
+            lev_tab(1)
+            lev_km(1)
+            for k in range(2, 9):
+                if k == 4:
+                    act(row("sr"), ["sr"], T.pb[:, 0:C], ["pb0"])
+                level(k)
+            if r == 0:
+                quant("vin", ["vin"], 128, "qv")
+            finish(r + 1)
+    def store(eng, out, src, keys):
+        op(eng, lambda: Q[eng].dma_start(out, src), keys, [], sem="outs", inc=16)
+    mm("pb", 0, "qv", 0, "qx3")
+    store("y", T.nl[:], T.nlr[0:128:16, :], ["nlr"])
+    store("y", T.oc[:], T.qx3[:, 0:C].bitcast(dt.uint8), ["qx3"])
+    act(row("ysb"), ["ysb"], T.pb[:, 0:C], ["pb0"])
+    for k in range(4):
+        store("y", T.osc[4 * k:4 * k + 4, :], T.qx3s[32 * k:32 * k + 4, 0:C], ["qx3s"])
+    store("s", T.y[:], row("ysb"), ["ysb"])
+    for s in SEMAPHORES:
+        if cnt[s] and known["g"].get(s, 0) < cnt[s]:
+            g.wait_ge(T.sem[s], cnt[s])

@@ -1,25 +1,25 @@
-from concourse.bass import DstId, RemoteDMATransfer
-from concourse.mybir import dt, AluOpType, AxisListType, ActivationFunctionType
+from concourse.mybir import dt, AluOpType, ActivationFunctionType
 
 C = 448
 TW = 28
 STEP = [1, 2, 3]
-F16 = "float16"
 SCRATCH = {}
 
 
 def _decl():
-    f32, bf = "float32", "bfloat16"
-    for n in ["k0", "k0m", "kc", "cpr", "ka", "kb", "kma", "kmb", "lraw", "ln", "cs", "cp", "rst", "sr", "sa", "pm", "cand",
-              "cm", "mu", "w", "sgn", "ck", "lck", "nlr", "ysb"]:
+    f32, bf, f16 = "float32", "bfloat16", "float16"
+    for n in ["k0", "k0m", "kc", "cpr", "ka", "kb", "kma", "kmb", "lraw", "ln", "cs", "sr", "sa", "cand", "mu", "nu", "sgn", "ck", "lck", "nlr", "ysb"]:
         SCRATCH[n] = ("sbuf", [128, C], f32)
-    for n in ["ra", "rb", "eq", "lrow", "drow", "plr", "str_", "lenr", "ar", "trow", "sw", "csr", "lnr", "srow", "brow", "lc",
-              "dq", "lt1", "lt2", "fmr", "mr"]:
+    for n in ["cp", "rst", "pm", "cm"]:
+        SCRATCH[n] = ("sbuf", [128, C + 8], f32)
+    for n in ["eq", "lrow", "plr", "tplr", "tcsr", "tlenr", "trow", "sw", "csr", "lnr", "srow", "brow", "lc", "fmr"]:
         SCRATCH[n] = ("sbuf", [128, C], bf)
+    SCRATCH["ar"] = ("sbuf", [128, C + 16], bf)
     SCRATCH["ramp"] = ("sbuf", [128, C + 16], bf)
-    SCRATCH["ca"] = ("sbuf", [128, C], F16)
-    SCRATCH["cb"] = ("sbuf", [128, C], F16)
-    SCRATCH["c4"] = ("sbuf", [128, 4 * C], F16)
+    SCRATCH["ro"] = ("sbuf", [128, 9 * C], bf)
+    SCRATCH["cc"] = ("sbuf", [128, 6 * C], f16)
+    SCRATCH["c2s"] = ("sbuf", [128, 2 * C], f16)
+    SCRATCH["c4s"] = ("sbuf", [128, 4 * C], f16)
     SCRATCH["gr"] = ("sbuf", [128, 4 * C], bf)
     for b in range(4):
         for n in ["fh", "ft", "fs"]:
@@ -33,15 +33,9 @@ def _decl():
     for n, w in [("wq", 512), ("qe", 512), ("qu", 128), ("qur", 128), ("qv", 128), ("qz", C)] + [("qx%d" % i, C) for i in range(4)] + [("lq%d" % i, C) for i in range(3)]:
         SCRATCH[n] = ("sbuf", [128, w], "float8_e4m3fn_x4")
         SCRATCH[n + "s"] = ("sbuf", [128, w], "uint8")
-    SCRATCH["fl_s"] = ("sbuf", [128, TW], "int32")
-    SCRATCH["ml_s"] = ("sbuf", [128, TW], "int32")
-    SCRATCH["pcol"] = ("sbuf", [128, 2], "int32")
-    SCRATCH["ofi"] = ("sbuf", [128, 8], "int32")
-    SCRATCH["ofu"] = ("sbuf", [128, 8], "uint16")
-    SCRATCH["col"] = ("sbuf", [128, 8], f32)
-    SCRATCH["tf"] = ("sbuf", [128, TW * 40], f32)
-    SCRATCH["ti"] = ("sbuf", [128, TW * 4], "int32")
-    SCRATCH["tu"] = ("sbuf", [128, TW * 24], "uint16")
+    for n, w, t in [("fl_s", TW, "int32"), ("ml_s", TW, "int32"), ("pq", TW, "int32"), ("pqm", TW, "int32"), ("ofq", TW, "uint16"), ("ofi", 8, "int32"), ("ofu", 8, "uint16"),
+                    ("col", 8, f32), ("tf", TW * 36, f32), ("ti", TW * 4, "int32"), ("tu", TW * 16, "uint16"), ("t16", 16, bf), ("la16", 16, bf), ("lb16", 16, bf), ("lc16", 16, bf)]:
+        SCRATCH[n] = ("sbuf", [128, w], t)
     for i in range(3):
         SCRATCH["sp%d" % i] = ("sbuf", [128, 3 * TW], "uint16")
         SCRATCH["sl%d" % i] = ("sbuf", [128, TW], "uint16")
@@ -54,10 +48,12 @@ def _decl():
 _decl()
 LOADS = ["dfl", "dml", "dx", "du", "dv", "dwc", "dws"]
 SEMAPHORES = ["cv", "cs_", "ct", "cg", "snt", "outs"] + LOADS + ["%s%d" % (n, i) for n in ("aq", "al", "aa") for i in range(3)]
-TF = {n: i for i, n in enumerate(["jt", "f", "m", "mj", "fm", "dfm", "t", "cs", "ln", "st", "pl", "d", "g0", "g1", "g2", "g3", "i0", "ng", "t1", "ii",
-                                  "pi", "u", "inv", "bq", "t2", "tp", "sw", "sg", "si", "lcur"])}
-TU = {n: i for i, n in enumerate(["tab%d" % k for k in range(9)] + ["m", "root", "d", "pl", "end", "l", "tp", "T", "sig", "b"])}
+TF = {n: i for i, n in enumerate(["jt", "f", "m", "mj", "fm", "dfm", "t", "t2x", "ln", "cs", "pl", "g0", "g1", "g2", "g3", "i0", "ng", "t1", "p0", "pi", "u", "inv", "bq",
+                                  "t2", "tp", "sw", "sg", "si", "sn", "e1", "wr", "wl", "pb"])}
+TU = {n: i for i, n in enumerate(["tab%d" % k for k in range(9)] + ["m", "root", "l", "tp", "T", "sig", "b"])}
 TI = {"k": 0, "root": 1, "d": 2, "n": 3}
+H, HW = 192, 12
+GAT, HALF, TINY, WAKE = 0.70, 0.38, 0.12, 0.06
 
 
 def rank_program(g, core, T, topo):
@@ -68,90 +64,57 @@ def rank_program(g, core, T, topo):
     AF = ActivationFunctionType
     Q = {"v": g.vector, "s": g.scalar, "t": g.tensor, "g": g, "y": g.sync}
     CS = {"v": "cv", "s": "cs_", "t": "ct", "g": "cg"}
-    cnt = {n: 0 for n in SEMAPHORES}
-    known = {e: {} for e in Q}
-    clock = {}
-    lastw, readers = {}, {}
+    prog = []
 
-    def need(eng, deps):
-        best = {}
-        for s, v in deps:
-            best[s] = max(best.get(s, 0), v)
-        own = CS.get(eng)
-        for s in sorted(best, key=lambda n: (n == own, n)):
-            v = best[s]
-            if known[eng].get(s, 0) >= v:
-                continue
-            Q[eng].wait_ge(T.sem[s], v)
-            for a, b in clock[(s, v)].items():
-                known[eng][a] = max(known[eng].get(a, 0), b)
-
-    def op(eng, fn, reads, writes, sem=None, inc=1):
-        deps = []
-        for k in reads:
-            if k in lastw:
-                deps.append(lastw[k])
-        for k in writes:
-            if k in lastw:
-                deps.append(lastw[k])
-            for d in readers.get(k, []):
-                deps.append(d)
-        need(eng, deps)
-        s = sem or CS[eng]
-        cnt[s] += inc
-        fn().then_inc(T.sem[s], inc)
-        me = (s, cnt[s])
-        clock[me] = dict(known[eng])
-        clock[me][s] = cnt[s]
-        for k in reads:
-            readers.setdefault(k, []).append(me)
-        for k in writes:
-            lastw[k] = me
-            readers[k] = []
-        return me
-
-    def arrive(sem, n, keys):
-        cnt[sem] += n
-        clock[(sem, n)] = {sem: n}
-        for k in keys:
-            lastw[k] = (sem, n)
-            readers[k] = []
+    def op(eng, fn, reads, writes, cost=TINY, sem=None, inc=1, lat=0.0, remote=None):
+        prog.append({"eng": eng, "fn": fn, "r": reads, "w": writes, "c": cost, "sem": sem, "inc": inc, "lat": lat, "remote": remote})
 
     tf = lambda n: T.tf[:, TW * TF[n]:TW * TF[n] + TW]
-    tu = lambda n: T.tu[:, TW * TU[n]:TW * TU[n] + TW]
+    tu = lambda n, a=0, b=TW: T.tu[:, TW * TU[n] + a:TW * TU[n] + b]
     ti = lambda n: T.ti[:, TW * TI[n]:TW * TI[n] + TW]
     cl = lambda i: T.col[:, i:i + 1]
-    row = lambda n: T[n][:, 0:C]
+    SLOT = {"%s%d" % (n, k): (m, C * k) for n, m, z in (("ro", "ro", 9), ("c", "cc", 6)) for k in range(z)}
 
-    def tt(out, wk, a, b, o, rk):
-        op("v", lambda: g.vector.tensor_tensor(out, a, b, o), rk, wk)
+    def row(n):
+        n, a = SLOT.get(n, (n, 0))
+        return T[n][:, a:a + C]
 
-    def ts(out, wk, a, s1, s2, o0, o1, rk):
+    def sampled(n):
+        n, a = SLOT.get(n, (n, 0))
+        return T[n][:, a + 15:a + C:16]
+
+    row1 = lambda n: T[n][:, 1:C + 1]
+    win1 = lambda n: T[n][:, 0:C + 1]
+
+    def tt(out, wk, a, b, o, rk, c=TINY):
+        op("v", lambda: g.vector.tensor_tensor(out, a, b, o), rk, wk, c)
+
+    def ts(out, wk, a, s1, s2, o0, o1, rk, c=TINY):
         if o1 is None:
-            op("v", lambda: g.vector.tensor_scalar(out, a, s1, None, o0), rk, wk)
+            op("v", lambda: g.vector.tensor_scalar(out, a, s1, None, o0), rk, wk, c)
         else:
-            op("v", lambda: g.vector.tensor_scalar(out, a, s1, s2, o0, o1), rk, wk)
+            op("v", lambda: g.vector.tensor_scalar(out, a, s1, s2, o0, o1), rk, wk, c)
 
-    def cp(out, wk, a, rk):
-        op("v", lambda: g.vector.tensor_copy(out, a), rk, wk)
+    def cp(out, wk, a, rk, c=TINY):
+        op("v", lambda: g.vector.tensor_copy(out, a), rk, wk, c)
 
-    def act(out, wk, a, rk, func=None, **kw):
-        op("s", lambda: g.scalar.activation(out, a, func or AF.Copy, **kw), rk, wk)
+    def act(out, wk, a, rk, c=GAT, func=None, **kw):
+        op("s", lambda: g.scalar.activation(out, a, func or AF.Copy, **kw), rk, wk, c)
 
-    def scan(out, wk, d0, d1, init, o0, o1, rk):
-        op("v", lambda: g.vector.tensor_tensor_scan(out, d0, d1, init, o0, o1), rk, wk)
+    def scan(out, wk, d0, d1, init, o0, o1, rk, c=0.43):
+        op("v", lambda: g.vector.tensor_tensor_scan(out, d0, d1, init, o0, o1), rk, wk, c)
 
-    def latch(rname, cname="ca", rap=None, cap=None, rk=None, wk=None):
-        scan(cap if cap is not None else row(cname), [wk or cname], rap if rap is not None else row(rname), row("lc"), -1024.0, A.max, A.add, [rk or rname, "lc"])
+    def latch(ap, rk, cap, wk):
+        scan(cap, [wk], ap, row("lc"), -1024.0, A.max, A.add, (rk if isinstance(rk, list) else [rk]) + ["lc"], 0.26)
 
     def tabs(cname, out, wk, col):
-        ts(out, wk, T[cname][:, 15:C:16], cl(col), None, A.add, None, [cname, "col%d" % col])
+        ts(out, wk, sampled(cname), cl(col), None, A.add, None, [cname, "col%d" % col])
 
     def tabm(cname, out, wk, col):
-        ts(out, wk, T[cname][:, 15:C:16], -1.0, cl(col), A.mult, A.add, [cname, "col%d" % col])
+        ts(out, wk, sampled(cname), -1.0, cl(col), A.mult, A.add, [cname, "col%d" % col])
 
     def load(eng, sem, out, src, key):
-        op(eng, lambda: Q[eng].dma_start(out, src), [], [key], sem=sem, inc=16)
+        op(eng, lambda: Q[eng].dma_start(out, src), [], [key], 0.07, sem=sem, inc=16, lat=2.0)
     load("y", "dfl", T.fl_s[:], T.fl[:], "fl_s")
     load("s", "dx", T.xin[:], T.x[:], "xin")
     load("y", "dml", T.ml_s[:], T.ml[:], "ml_s")
@@ -160,287 +123,342 @@ def rank_program(g, core, T, topo):
     load("y", "dws", T.wqs[:, 0:512], T.ws[:], "wqs")
     load("y", "dv", T.vin[:], T.v[:], "vin")
 
-    op("g", lambda: g.iota(T.pcol[:, 0:1], [[0, 1]], 0, 1), [], ["pcol"])
-    op("g", lambda: g.iota(row("dq"), [[0, TW], [1, 16]], 0, 0, allow_small_or_imprecise_dtypes=True), [], ["dq"])
-    op("g", lambda: g.iota(T.ramp[:], [[1, C + 16]], -224, 0, allow_small_or_imprecise_dtypes=True), [], ["ramp"])
-    op("g", lambda: g.iota(row("k0"), [[512, C]], 0, 0, allow_small_or_imprecise_dtypes=True), [], ["k0"])
-    op("g", lambda: g.iota(tf("jt"), [[16, TW]], 0, 0, allow_small_or_imprecise_dtypes=True), [], ["tf.jt"])
-    op("g", lambda: g.iota(T.ofi[:], [[16, 8]], 0, 0), [], ["ofi"])
-    op("g", lambda: g.iota(row("cpr"), [[-1, C]], 449, 0, allow_small_or_imprecise_dtypes=True), [], ["cpr"])
-    ts(T.pcol[:, 1:2], ["pc1"], T.pcol[:, 0:1], 15, None, A.bitwise_and, None, ["pcol"])
-    cp(cl(0), ["col0"], T.pcol[:, 1:2], ["pc1"])
-    ts(row("dq"), ["dq"], row("dq"), cl(0), None, A.subtract, None, ["dq", "col0"])
-    ts(row("lt1"), ["lt1"], row("dq"), 0.0, -1024.0, A.is_lt, A.mult, ["dq"])
-    ts(row("lt2"), ["lt2"], row("dq"), 0.0, 512.0, A.is_equal, A.mult, ["dq"])
-    tt(row("lt1"), ["lt1"], row("lt1"), row("lt2"), A.add, ["lt1", "lt2"])
-    ts(row("lt2"), ["lt2"], row("dq"), 15.0, -1024.0, A.is_equal, A.mult, ["dq"])
-    tt(row("lc"), ["lc"], row("lt1"), row("lt2"), A.add, ["lt1", "lt2"])
+    def iota(out, wk, pattern, base, cm, n, flag=True):
+        c = 0.15 + 0.00166 * n
+        if flag:
+            op("g", lambda: g.iota(out, pattern, base, cm, allow_small_or_imprecise_dtypes=True), [], wk, c)
+        else:
+            op("g", lambda: g.iota(out, pattern, base, cm), [], wk, c)
+    iota(T.pq[:], ["pq"], [[0, TW]], 0, 1, TW, False)
+    iota(T.t16[:], ["t16"], [[1, 16]], 0, 0, 16)
+    iota(T.ramp[:], ["ramp"], [[1, C + 16]], -224, 0, C + 16)
+    iota(row("k0"), ["k0"], [[512, C]], 0, 0, C)
+    iota(row("k0m"), ["k0m"], [[512, C]], -1, 0, C)
+    iota(tf("jt"), ["jt0"], [[16, TW]], 0, 0, TW)
+    iota(T.ofi[:], ["ofi"], [[16, 8]], 0, 0, 8, False)
+    iota(row("cpr"), ["cpr"], [[-1, C]], 449, 0, C)
+    iota(row("kc"), ["kc"], [[512, C]], -512, 0, C)
+    ts(T.pqm[:], ["pqm"], T.pq[:], 15, None, A.bitwise_and, None, ["pq"])
+    cp(cl(0), ["col0"], T.pqm[:, 0:1], ["pqm"])
+    cp(T.ofq[:], ["ofq"], T.pqm[:], ["pqm"])
+    ts(T.t16[:], ["t16"], T.t16[:], cl(0), None, A.subtract, None, ["t16", "col0"])
+    ts(T.la16[:], ["la16"], T.t16[:], 0.0, -1024.0, A.is_lt, A.mult, ["t16"])
+    ts(T.lb16[:], ["lb16"], T.t16[:], 0.0, 512.0, A.is_equal, A.mult, ["t16"])
+    tt(T.la16[:], ["la16"], T.la16[:], T.lb16[:], A.add, ["la16", "lb16"])
+    ts(T.lb16[:], ["lb16"], T.t16[:], 15.0, -1024.0, A.is_equal, A.mult, ["t16"])
+    tt(T.lc16[:], ["lc16"], T.la16[:], T.lb16[:], A.add, ["la16", "lb16"])
+    act(row("lc"), ["lc"], T.lc16[:].indirect(T.ofq[:]), ["lc16", "ofq"])
+    act(row("lck"), ["lck"], row("lc"), ["lc"], 0.43, scale=512.0)
     ts(cl(1), ["col1"], cl(0), 0.0, 1024.0, A.is_equal, A.mult, ["col0"])
     ts(cl(1), ["col1"], cl(1), -512.0, None, A.add, None, ["col1"])
     ts(cl(2), ["col2"], cl(1), 224.0, None, A.add, None, ["col1"])
+    ts(cl(3), ["col3"], cl(1), 512.0, 511.0, A.mult, A.add, ["col1"])
+    ts(cl(6), ["col6"], cl(1), 511.0 / 512 - 0.499, None, A.add, None, ["col1"])
+    ts(cl(4), ["col4"], cl(1), -1.0, 449.0, A.mult, A.add, ["col1"])
+    ts(cl(5), ["col5"], cl(1), -1.0, 224.0, A.mult, A.add, ["col1"])
+    for n in ["cp", "rst", "pm", "cm"]:
+        op("v", lambda n=n: g.vector.memset(T[n][:, 0:1], 0.0), [], [n + "0"])
+    op("v", lambda: g.vector.memset(T.ar[:, 0:1], 0.0), [], ["ar0"])
+    op("v", lambda: g.vector.memset(T.et[:], 1.0), [], ["et1"], 0.5)
+    op("g", lambda: g.affine_select(T.et[:], T.et[:], [[-1, 4], [1, 512]], A.is_equal, 0.0, 0, -4), ["et1"], ["et"], 3.6)
     cp(tu("tab0"), ["tu.tab0"], T.fl_s[:], ["fl_s"])
-    ts(row("k0m"), ["k0m"], row("k0"), -1.0, None, A.add, None, ["k0"])
 
-    rows = ["ra", "rb"]
     KS, KM = ["ka", "kb"], ["kma", "kmb"]
 
     def frow():
-        act(row("ra"), ["ra"], T.ramp[:].indirect(tu("tab0")), ["ramp", "tu.tab0"])
+        act(row("ro0"), ["ro0"], T.ramp[:].indirect(tu("tab0")), ["ramp", "tu.tab0"])
 
-    def lev_row(k):
-        a, b = rows[k % 2], rows[(k + 1) % 2]
-        act(row(b), [b], row(a).indirect(tu("tab%d" % k)), [a, "tu.tab%d" % k])
-
-    def lev_key(k):
-        src = "k0" if k == 0 else KS[k % 2]
-        sm = "k0m" if k == 0 else KM[k % 2]
-        dst = KS[(k + 1) % 2]
-        tt(row(dst), [dst], row(src).indirect(tu("tab%d" % k)), row(sm), A.min, [src, sm, "tu.tab%d" % k])
-
-    def lev_tab(k):
-        b = rows[(k + 1) % 2]
-        latch(b, "ca")
-        tabs("ca", tu("tab%d" % (k + 1)), ["tu.tab%d" % (k + 1)], 2)
-
-    def lev_km(k):
-        a = KS[(k + 1) % 2]
-        m = KM[(k + 1) % 2]
-        act(row(m), [m], row(a), [a], func=AF.Copy, bias=-float(2 ** (k + 1)))
-
-    def level(k):
-        if k < 8:
-            lev_row(k)
-        lev_key(k)
-        if k < 8:
-            lev_tab(k)
-            lev_km(k)
+    def levels():
+        for k in range(9):
+            if k < 8:
+                a, b = "ro%d" % k, "ro%d" % (k + 1)
+                act(row(b), [b], row(a).indirect(tu("tab%d" % k)), [a, "tu.tab%d" % k])
+            src = "k0" if k == 0 else KS[k % 2]
+            sm = "k0m" if k == 0 else KM[k % 2]
+            dst, dm = KS[(k + 1) % 2], KM[(k + 1) % 2]
+            tt(row(dst), [dst], row(src).indirect(tu("tab%d" % k)), row(sm), A.min, [src, sm, "tu.tab%d" % k], GAT)
+            if k < 8:
+                c = "c%d" % (k % 2)
+                latch(row(b), b, row(c), c)
+                tabs(c, tu("tab%d" % (k + 1)), ["tu.tab%d" % (k + 1)], 2)
+                act(row(dm), [dm], row(dst), [dst], 0.43, bias=-float(2 ** (k + 1)))
 
     KF = KS[1]
 
-    def send(dst_name, src_name, sem, code=False, w=C):
-        dst = T.cores[rank ^ STEP[cur[0]]]
+    def send(r, dst_name, src_name, rk, sem, code=False, w=C):
+        dst = T.cores[rank ^ STEP[r]]
         rid, pid = topo.addr(dst)[0:2]
         m = topo.mask(core, dst)
+        n = len(topo.engines(core, dst))
         if code:
             o, i = T[dst_name][:, 0:w].bitcast(dt.uint8), T[src_name][:, 0:w].bitcast(dt.uint8)
         else:
             o, i = T[dst_name][:, 0:w], T[src_name][:, 0:w]
-        need("g", [lastw[src_name]])
-        n = len(topo.engines(core, dst))
-        cnt["snt"] += n
-        g.remote_dma(out_ap=o, in_ap=i, remote_sem=T.sem[sem], local_sem=T.sem.snt, pid=pid, routing_id=rid, dma_engine_mask=m)
-        return n
-
-    cur = [0]
+        op("g", lambda: g.remote_dma(out_ap=o, in_ap=i, remote_sem=T.sem[sem], local_sem=T.sem.snt, pid=pid, routing_id=rid, dma_engine_mask=m),
+           rk, [dst_name], 0.5, lat=4.0 + (6.0 if code else 0.0), remote=(sem, n))
 
     def finish(r):
+        sp, sl = "sp%d" % r, "sl%d" % r
+        tt(row("lraw"), ["lraw"], row(KF).indirect(tu("tab0")), row("kc"), A.subtract, [KF, "tu.tab0", "kc"], GAT)
+        act(row("ln"), ["ln"], row("lraw"), ["lraw"], 0.43, func=AF.Relu)
         scan(row("ck"), ["ck"], row(KF), row("lck"), -524288.0, A.max, A.add, [KF, "lck"])
         ts(ti("k"), ["ti.k"], T.ck[:, 15:C:16], cl(3), None, A.add, None, ["ck", "col3"])
-        ts(ti("root"), ["ti.root"], ti("k"), 9, None, A.arith_shift_right, None, ["ti.k"])
-        tt(row("lraw"), ["lraw"], row(KF).indirect(tu("tab0")), row("kc"), A.subtract, [KF, "tu.tab0", "kc"])
+        ts(ti("root"), ["ti.root"], T.ck[:, 15:C:16], 2.0 ** -9, cl(6), A.mult, A.add, ["ck", "col6"])
         cp(tu("root"), ["tu.root"], ti("root"), ["ti.root"])
-        act(row("ln"), ["ln"], row("lraw"), ["lraw"], func=AF.Relu)
         ts(ti("d"), ["ti.d"], ti("k"), 511, None, A.bitwise_and, None, ["ti.k"])
-        cp(tu("d"), ["tu.d"], ti("d"), ["ti.d"])
-        cp(tf("d"), ["tf.d"], ti("d"), ["ti.d"])
-        act(row("lnr"), ["lnr"], row("ln").indirect(tu("root")), ["ln", "tu.root"], func=AF.Copy, bias=-224.0)
+        act(row("lnr"), ["lnr"], row("lraw").indirect(tu("root")), ["lraw", "tu.root"], bias=-224.0)
         scan(row("cs"), ["cs"], row("ln"), row("ln"), 0.0, A.add, A.max, ["ln"])
-        ts(row("csr"), ["csr"], row("cs").indirect(tu("root")), -224.0, None, A.add, None, ["cs", "tu.root"])
-        latch("lnr", "ca")
-        latch("csr", "cb")
-        tabs("ca", tf("ln"), ["tf.ln"], 2)
-        tabs("cb", tf("cs"), ["tf.cs"], 2)
-        tt(tf("st"), ["tf.st"], tf("cs"), tf("ln"), A.subtract, ["tf.cs", "tf.ln"])
-        tt(tf("pl"), ["tf.pl"], tf("st"), tf("d"), A.add, ["tf.st", "tf.d"])
-        cp(tu("pl"), ["tu.pl"], tf("pl"), ["tf.pl"])
-        sp = "sp%d" % r
-        op("v", lambda: g.vector.tensor_copy(row("cp").indirect(tu("pl")), row("cpr")), ["cpr", "tu.pl"], ["cp"])
-        cp(T[sp][:, 0:TW], [sp], tf("pl"), ["tf.pl"])
-        cp(T[sp][:, TW:2 * TW], [sp + "b"], tf("st"), ["tf.st"])
-        cp(T[sp][:, 2 * TW:3 * TW], [sp], tf("ln"), ["tf.ln", sp + "b"])
-        ts(tu("end"), ["tu.end"], tf("cs"), -1.0, None, A.add, None, ["tf.cs"])
-        arrive("al%d" % r, send("lp%d" % r, sp, "al%d" % r, w=3 * TW), ["lp%d" % r])
-        latch("cp", "ca")
-        sl = "sl%d" % r
-        tabm("ca", T[sl][:], [sl], 4)
-        arrive("aa%d" % r, send("la%d" % r, sl, "aa%d" % r, w=TW), ["la%d" % r])
-
-    def sendx(r):
-        cur[0] = r
-        n = send("lq%d" % r, "qx%d" % r, "aq%d" % r, code=True)
-        n += send("lq%ds" % r, "qx%ds" % r, "aq%d" % r)
-        arrive("aq%d" % r, n, ["lq%d" % r, "lq%ds" % r])
+        ts(row("csr"), ["csr"], row("cs").indirect(tu("root")), -224.0, None, A.add, None, ["cs", "tu.root"], GAT)
+        latch(row("lnr"), "lnr", T.c2s[:, 0:C], "c2a")
+        latch(row("csr"), "csr", T.c2s[:, C:2 * C], "c2b")
+        ts(T.tf[:, TW * TF["ln"]:TW * (TF["ln"] + 2)], ["tf.lc"], T.c2s[:, 15:2 * C:16], cl(2), None, A.add, None, ["c2a", "c2b", "col2"])
+        tt(tf("pl"), ["tf.pl"], tf("cs"), ti("d"), A.subtract, ["tf.lc", "ti.d"])
+        cp(T[sp][:, 0:TW], [sp + "a"], tf("pl"), ["tf.pl"])
+        op("v", lambda: g.vector.tensor_copy(win1("cp").indirect(T[sp][:, 0:TW]), row("cpr")), ["cpr", sp + "a", "cp0"], ["cp"], 1.5)
+        cp(T[sp][:, TW:3 * TW], [sp + "b"], T.tf[:, TW * TF["ln"]:TW * (TF["ln"] + 2)], ["tf.lc"])
+        send(r, "lp%d" % r, sp, [sp + "a", sp + "b"], "al%d" % r, w=3 * TW)
+        latch(row1("cp"), "cp", row("c4"), "c4")
+        tabm("c4", T[sl][:], [sl], 4)
+        send(r, "la%d" % r, sl, [sl], "aa%d" % r, w=TW)
 
     def mm(dst, b, st, so, mv):
         op("t", lambda: g.tensor.matmul_mx(T[dst][:, 512 * b:512 * b + C], T[st][:, so:so + 128], T[st + "s"][:, so:so + 128], T[mv][:, 0:C], T[mv + "s"][:, 0:C], True, True),
-           [st, st + "s", mv, mv + "s"], [dst + str(b)])
+           [st, st + "s", mv, mv + "s"], [dst + str(b)], 0.4)
 
     def quant(tile, keys, w, q):
-        op("v", lambda: g.vector.quantize_mx(T[q][:, 0:w], T[q + "s"][:, 0:w], T[tile][:, 0:4 * w]), keys, [q, q + "s"])
+        op("v", lambda: g.vector.quantize_mx(T[q][:, 0:w], T[q + "s"][:, 0:w], T[tile][:, 0:4 * w]), keys, [q, q + "s"], 0.08 + 0.00088 * w)
 
-    def scores(r):
+    def state_made(r):
+        send(r, "lq%d" % r, "qx%d" % r, ["qx%d" % r], "aq%d" % r, code=True)
+        send(r, "lq%ds" % r, "qx%ds" % r, ["qx%ds" % r], "aq%d" % r)
         mm("pb", 0, "qur", 0, "qx%d" % r)
+        act(row("sr"), ["sr"], T.pb[:, 0:C], ["pb0"], 0.43)
         for b in range(4):
             mm("pa", b, "qe", 128 * b, "qx%d" % r)
+        for b in range(4):
+            mm("pb", b, "qe", 128 * b, "lq%d" % r)
 
     frow()
-    level(0)
-    op("v", lambda: g.vector.memset(T.et[:], 1.0), [], ["et"])
-    op("g", lambda: g.affine_select(T.et[:], T.et[:], [[-1, 4], [1, 512]], A.is_equal, 0.0, 0, -4), ["et"], ["et"])
+    levels()
     cp(tu("m"), ["tu.m"], T.ml_s[:], ["ml_s"])
     cp(tf("f"), ["tf.f"], T.fl_s[:], ["fl_s"])
     cp(tf("m"), ["tf.m"], T.ml_s[:], ["ml_s"])
-    act(row("fmr"), ["fmr"], row("ra").indirect(tu("m")), ["ra", "tu.m"])
-    act(row("mr"), ["mr"], T.ramp[:].indirect(tu("m")), ["ramp", "tu.m"])
-    ts(cl(3), ["col3"], cl(1), 512.0, 511.0, A.mult, A.add, ["col1"])
-    ts(cl(4), ["col4"], cl(1), -1.0, 449.0, A.mult, A.add, ["col1"])
-    ts(cl(5), ["col5"], cl(1), -1.0, 224.0, A.mult, A.add, ["col1"])
-    level(1)
-    ts(row("lck"), ["lck"], row("lc"), 512.0, None, A.mult, None, ["lc"])
-    level(2)
+    act(row("fmr"), ["fmr"], row("ro0").indirect(tu("m")), ["ro0", "tu.m"])
+    latch(row("fmr"), "fmr", row("c2"), "c2")
+    tabs("c2", tf("fm"), ["tf.fm"], 2)
+    tt(tf("dfm"), ["tf.dfm"], tf("fm"), tf("f"), A.subtract, ["tf.fm", "tf.f"])
+    ts(tf("jt"), ["tf.jt"], tf("jt"), cl(0), None, A.add, None, ["jt0", "col0"])
+    tt(tf("mj"), ["tf.mj"], tf("m"), tf("jt"), A.subtract, ["tf.m", "tf.jt"])
+    ts(tf("sn"), ["tf.sn"], tf("mj"), 0.0, 2.0, A.is_gt, A.mult, ["tf.mj"])
+    ts(tu("sig"), ["tu.sig"], tf("sn"), 223.0, None, A.add, None, ["tf.sn"])
+    act(row("sgn"), ["sgn"], T.ramp[:].indirect(tu("sig")), ["ramp", "tu.sig"])
     quant("xin", ["xin"], C, "qx0")
-    sendx(0)
-    level(3)
     quant("uin", ["uin"], 128, "qu")
     cp(T.ofu[:], ["ofu"], T.ofi[:], ["ofi"])
-    op("v", lambda: g.vector.tensor_copy(T.qur[:, 0:128].bitcast(dt.uint32), T.qu[:, 0:128].bitcast(dt.uint32).indirect(T.ofu[:, 0:8])), ["qu", "ofu"], ["qur"])
-    op("v", lambda: g.vector.tensor_copy(T.qurs[:, 0:128], T.qus[:, 0:128].indirect(T.ofu[:, 0:8])), ["qus", "ofu"], ["qurs"])
-    level(4)
+    op("v", lambda: g.vector.tensor_copy(T.qur[:, 0:128].bitcast(dt.uint32), T.qu[:, 0:128].bitcast(dt.uint32).indirect(T.ofu[:, 0:8])), ["qu", "ofu"], ["qur"], 0.27)
+    op("s", lambda: g.scalar.activation(T.qurs[:, 0:128], T.qus[:, 0:128].indirect(T.ofu[:, 0:8]), AF.Copy), ["qus", "ofu"], ["qurs"], 0.27)
     quant("et", ["et"], 512, "qe")
-    scores(0)
-    ts(row("kc"), ["kc"], row("k0"), -512.0, None, A.add, None, ["k0"])
-    level(5)
-    latch("fmr", "cb")
-    tabs("cb", tf("fm"), ["tf.fm"], 2)
-    tt(tf("dfm"), ["tf.dfm"], tf("fm"), tf("f"), A.subtract, ["tf.fm", "tf.f"])
-    ts(tf("jt"), ["tf.jt"], tf("jt"), cl(0), None, A.add, None, ["tf.jt", "col0"])
-    tt(tf("mj"), ["tf.mj"], tf("m"), tf("jt"), A.subtract, ["tf.m", "tf.jt"])
-    level(6)
-    tt(row("sgn"), ["sgn"], row("mr"), T.ramp[:, 0:C], A.is_gt, ["mr", "ramp"])
-    ts(row("sgn"), ["sgn"], row("sgn"), 2.0, -1.0, A.mult, A.add, ["sgn"])
-    level(7)
-    act(row("sr"), ["sr"], T.pb[:, 0:C], ["pb0"])
-    level(8)
+    state_made(0)
     finish(0)
+    ts(tf("e1"), ["tf.e1"], ti("d"), 1.0, None, A.add, None, ["ti.d"])
+    tt(tf("wr"), ["tf.wr"], tf("e1"), tf("ln"), A.is_equal, ["tf.e1", "tf.lc"])
+    tt(tf("wl"), ["tf.wl"], tf("wr"), tf("ln"), A.mult, ["tf.wr", "tf.lc"])
+    tt(tf("pb"), ["tf.pb"], tf("pl"), tf("wl"), A.add, ["tf.pl", "tf.wl"])
+    ts(tu("b"), ["tu.b"], tf("pb"), -1.0, None, A.add, None, ["tf.pb"])
+    act(row("brow"), ["brow"], win1("cp").indirect(tu("b")), ["cp", "tu.b"], scale=-1.0, bias=225.0)
+    latch(row("brow"), "brow", row("c3"), "c3")
+    tabs("c3", tu("b"), ["tu.b"], 2)
 
+    grs = lambda i: T.gr[:, C * i:C * i + C]
+    c4s = lambda i: T.c4s[:, C * i:C * i + C]
     for r in range(3):
-        cur[0] = r
-        lq, sl, lp, la = "lq%d" % r, "sl%d" % r, "lp%d" % r, "la%d" % r
-        act(row("rst"), ["rst"], row("ln").indirect(T[sl][:]), ["ln", sl], func=AF.Copy, scale=-float(2 ** 90))
-        cp(row("sa"), ["sa"], row("sr").indirect(T[sl][:]), ["sr", sl])
-        scan(row("pm"), ["pm"], row("rst"), row("sa"), 0.0, A.add, A.max, ["rst", "sa"])
-        tt(row("eq"), ["eq"], row("pm").indirect(tu("end")), row("sr"), A.is_equal, ["pm", "tu.end", "sr"])
-        act(row("drow"), ["drow"], T.ramp[:].indirect(tu("d")), ["ramp", "tu.d"])
+        sl, lp, la, sp = "sl%d" % r, "lp%d" % r, "la%d" % r, "sp%d" % r
+        last = r == 2
+        end = T[sp][:, 2 * TW:3 * TW]
+        act(row1("rst"), ["rst"], row("ln").indirect(T[sl][:]), ["ln", sl, "rst0"], scale=-float(2 ** 90))
+        cp(row("sa"), ["sa"], row("sr").indirect(T[sl][:]), ["sr", sl], GAT)
+        scan(row1("pm"), ["pm"], row("rst"), row("sa"), -float(2 ** 90), A.add, A.max, ["rst", "rst0", "sa", "pm0"])
+        tt(row("eq"), ["eq"], win1("pm").indirect(end), row("sr"), A.is_equal, ["pm", sp + "b", "sr"], GAT)
+        tt(row("cand"), ["cand"], row("eq").indirect(T[sl][:]), row1("cp"), A.mult, ["eq", sl, "cp"], GAT)
+        scan(row1("cm"), ["cm"], row("rst"), row("cand"), 0.0, A.add, A.max, ["rst", "cand", "cm0"])
+        act(T.lrow[:, 0:H], ["lrowa"], win1("cm").indirect(T[sp][:, 2 * TW:2 * TW + HW]), ["cm", sp + "b"], HALF, bias=-225.0)
+        ts(T.lrow[:, H:C], ["lrowb"], win1("cm").indirect(T[sp][:, 2 * TW + HW:3 * TW]), -225.0, None, A.add, None, ["cm", sp + "b"], HALF)
+        latch(row("lrow"), ["lrowa", "lrowb"], row("c5"), "c5")
+        tabm("c5", tu("l"), ["tu.l"], 5)
+        act(row("plr"), ["plr"], T.ramp[:].indirect(T[sp][:, 0:TW]), ["ramp", sp + "a"])
         for b in range(4):
-            mm("pb", b, "qe", 128 * b, lq)
-            act(row("fh%d" % b), ["fh%d" % b], T.pa[:, 512 * b:512 * b + C], ["pa%d" % b], func=AF.Copy, scale=0.5)
-        tt(row("cand"), ["cand"], row("eq").indirect(T[sl][:]), row("cp"), A.mult, ["eq", sl, "cp"])
-        scan(row("cm"), ["cm"], row("rst"), row("cand"), 0.0, A.add, A.max, ["rst", "cand"])
-        ts(row("lrow"), ["lrow"], row("cm").indirect(tu("end")), -225.0, None, A.add, None, ["cm", "tu.end"])
-        latch("lrow", "ca")
-        tabm("ca", tu("l"), ["tu.l"], 5)
-        act(row("str_"), ["str_"], T.ramp[:].indirect(T[lp][:, TW:2 * TW]), ["ramp", lp])
-        act(row("lenr"), ["lenr"], T.ramp[:].indirect(T[lp][:, 2 * TW:3 * TW]), ["ramp", lp])
-        act(row("plr"), ["plr"], T.ramp[:].indirect(T[lp][:, 0:TW]), ["ramp", lp])
-        grs = lambda i: T.gr[:, C * i:C * i + C]
-        c4s = lambda i: T.c4[:, C * i:C * i + C]
-        cp(grs(2), ["gr2"], row("str_").indirect(tu("l")), ["str_", "tu.l"])
-        act(grs(1), ["gr1"], row("drow").indirect(tu("l")), ["drow", "tu.l"])
-        act(grs(0), ["gr0"], row("plr").indirect(tu("l")), ["plr", "tu.l"])
-        cp(grs(3), ["gr3"], row("lenr").indirect(tu("l")), ["lenr", "tu.l"])
-        act(row("ar"), ["ar"], T.ramp[:].indirect(T[la][:]), ["ramp", la])
-        for i in (2, 1, 3, 0):
-            latch(None, rap=grs(i), cap=c4s(i), rk="gr%d" % i, wk="c4%d" % i)
-        ts(T.tf[:, TW * TF["g0"]:TW * (TF["g0"] + 4)], ["tf.g"], T.c4[:, 15:4 * C:16], cl(2), None, A.add, None, ["c40", "c41", "c42", "c43", "col2"])
+            act(row("fh%d" % b), ["fh%d" % b], T.pa[:, 512 * b:512 * b + C], ["pa%d" % b], 0.43, scale=0.5)
+        act(row("tcsr"), ["tcsr"], T.ramp[:].indirect(T[lp][:, 2 * TW:3 * TW]), ["ramp", lp])
+        act(row("tlenr"), ["tlenr"], T.ramp[:].indirect(T[lp][:, TW:2 * TW]), ["ramp", lp])
+        act(row("tplr"), ["tplr"], T.ramp[:].indirect(T[lp][:, 0:TW]), ["ramp", lp])
+        cp(grs(3), ["gr3"], row("tlenr").indirect(tu("l")), ["tlenr", "tu.l"], GAT)
+        act(grs(1), ["gr1"], row("plr").indirect(tu("l")), ["plr", "tu.l"])
+        cp(grs(2), ["gr2"], row("tcsr").indirect(tu("l")), ["tcsr", "tu.l"], GAT)
+        act(grs(0), ["gr0"], row("tplr").indirect(tu("l")), ["tplr", "tu.l"])
+        act(row1("ar"), ["ar"], T.ramp[:].indirect(T[la][:]), ["ramp", la, "ar0"])
+        for i in (3, 1, 2, 0):
+            latch(grs(i), "gr%d" % i, c4s(i), "c4s%d" % i)
+        ts(T.tf[:, TW * TF["g0"]:TW * (TF["g0"] + 4)], ["tf.g"], T.c4s[:, 15:4 * C:16], cl(2), None, A.add, None, ["c4s0", "c4s1", "c4s2", "c4s3", "col2"], 0.15)
         for b in range(4):
-            act(row("ft%d" % b), ["ft%d" % b], T.pb[:, 512 * b:512 * b + C], ["pb%d" % b], func=AF.Copy, scale=0.5)
-        op("v", lambda: g.vector.reciprocal(tf("inv"), tf("g3")), ["tf.g"], ["tf.inv"])
-        tt(tf("i0"), ["tf.i0"], tf("g1"), tf("d"), A.subtract, ["tf.g", "tf.d"])
+            act(row("ft%d" % b), ["ft%d" % b], T.pb[:, 512 * b:512 * b + C], ["pb%d" % b], 0.43, scale=0.5)
+        op("v", lambda: g.vector.reciprocal(tf("inv"), tf("g3")), ["tf.g"], ["tf.inv"], 0.35)
+        tt(tf("i0"), ["tf.i0"], tf("pl"), tf("g1"), A.subtract, ["tf.g", "tf.pl"])
         ts(tf("ng"), ["tf.ng"], tf("i0"), 0.0, None, A.is_lt, None, ["tf.i0"])
-        tt(tf("pi"), ["tf.pi"], tf("g0"), tf("i0"), A.subtract, ["tf.g", "tf.i0"])
-        tt(tf("t1"), ["tf.t1"], tf("ng"), tf("ln"), A.mult, ["tf.ng", "tf.ln"])
-        tt(tf("pi"), ["tf.pi"], tf("pi"), tf("t1"), A.subtract, ["tf.pi", "tf.t1"])
-        tt(tf("u"), ["tf.u"], tf("pi"), tf("g2"), A.subtract, ["tf.pi", "tf.g"])
+        tt(tf("p0"), ["tf.p0"], tf("g0"), tf("i0"), A.add, ["tf.g", "tf.i0"])
+        tt(tf("t1"), ["tf.t1"], tf("ng"), tf("ln"), A.mult, ["tf.ng", "tf.lc"])
+        tt(tf("pi"), ["tf.pi"], tf("p0"), tf("t1"), A.add, ["tf.p0", "tf.t1"])
+        tt(tf("u"), ["tf.u"], tf("g2"), tf("pi"), A.subtract, ["tf.pi", "tf.g"])
         tt(tf("bq"), ["tf.bq"], tf("u"), tf("inv"), A.mult, ["tf.u", "tf.inv"])
         ts(ti("n"), ["ti.n"], tf("bq"), -0.4989, None, A.add, None, ["tf.bq"])
         tt(tf("t2"), ["tf.t2"], ti("n"), tf("g3"), A.mult, ["ti.n", "tf.g"])
-        tt(tf("tp"), ["tf.tp"], tf("pi"), tf("t2"), A.subtract, ["tf.pi", "tf.t2"])
+        tt(tf("tp"), ["tf.tp"], tf("pi"), tf("t2"), A.add, ["tf.pi", "tf.t2"])
         cp(tu("tp"), ["tu.tp"], tf("tp"), ["tf.tp"])
-        cp(row("trow"), ["trow"], row("ar").indirect(tu("tp")), ["ar", "tu.tp"])
-        latch("trow", "ca")
-        tabs("ca", tu("T"), ["tu.T"], 2)
-        tt(row("mu"), ["mu"], row("sr").indirect(tu("T")), row("sgn"), A.mult, ["sr", "tu.T", "sgn"])
+        act(T.trow[:, 0:H], ["trowa"], win1("ar").indirect(tu("tp", 0, HW)), ["ar", "tu.tp"], HALF)
+        cp(T.trow[:, H:C], ["trowb"], win1("ar").indirect(tu("tp", HW)), ["ar", "tu.tp"], HALF)
+        latch(row("trow"), ["trowa", "trowb"], row("c5"), "c5")
+        tabs("c5", tu("T"), ["tu.T"], 2)
+        tt(row("mu"), ["mu"], row("sr").indirect(tu("T")), row("sgn"), A.mult, ["sr", "tu.T", "sgn"], GAT)
         for b in range(4):
             act(row("fs%d" % b), ["fs%d" % b], row("ft%d" % b).indirect(tu("T")), ["ft%d" % b, "tu.T"])
-            if b == 0:
-                act(row("w"), ["w"], row("mu"), ["mu"], func=AF.Copy, scale=-1.0)
-        tt(row("sw"), ["sw"], row("mu").indirect(tu("m")), row("w"), A.is_lt, ["mu", "w", "tu.m"])
-        latch("sw", "ca")
-        tabs("ca", tf("sw"), ["tf.sw"], 1)
+        act(row("nu"), ["nu"], row("mu"), ["mu"], 0.43, scale=-1.0)
+        tt(row("sw"), ["sw"], row("mu").indirect(tu("m")), row("nu"), A.is_lt, ["mu", "nu", "tu.m"], GAT)
+        latch(row("sw"), "sw", row("c5"), "c5")
+        tabs("c5", tf("sw"), ["tf.sw"], 1)
         tt(tf("t"), ["tf.t"], tf("sw"), tf("dfm"), A.mult, ["tf.sw", "tf.dfm"])
         tt(tf("f"), ["tf.f"], tf("f"), tf("t"), A.add, ["tf.f", "tf.t"])
         cp(tu("tab0"), ["tu.tab0"], tf("f"), ["tf.f"])
-        last = r == 2
-        if not last:
-            frow()
-            lev_row(0)
-        else:
-            act(row("nlr"), ["nlr"], T.ramp[:].indirect(tu("tab0")), ["ramp", "tu.tab0"], func=AF.Copy, bias=224.0)
         for b in range(4):
-            tt(T.zt[:, b:4 * C:4], ["zt%d" % b], row("fh%d" % b).indirect(tu("tab0")), row("fs%d" % b), A.add, ["fh%d" % b, "fs%d" % b, "tu.tab0"])
-            if b == 0 and r > 0:
-                tt(tf("sg"), ["tf.sg"], tf("sw"), tf("mj"), A.mult, ["tf.sw", "tf.mj"])
-            if b == 1 and r > 0:
-                tt(tf("si"), ["tf.si"], tf("sg"), tf("jt"), A.add, ["tf.sg", "tf.jt"])
-            if b == 2 and r > 0:
-                cp(tu("sig"), ["tu.sig"], tf("si"), ["tf.si"])
+            tt(T.zt[:, b:4 * C:4], ["zt%d" % b], row("fh%d" % b).indirect(tu("tab0")), row("fs%d" % b), A.add, ["fh%d" % b, "fs%d" % b, "tu.tab0"], GAT)
         quant("zt", ["zt0", "zt1", "zt2", "zt3"], C, "qz")
         for b in range(4):
             mm("pa", b, "wq", 128 * b, "qz")
+        tt(tf("sg"), ["tf.sg"], tf("sw"), tf("mj"), A.mult, ["tf.sw", "tf.mj"])
+        tt(tf("si"), ["tf.si"], tf("sg"), tf("jt"), A.add, ["tf.sg", "tf.jt"])
+        cp(tu("sig"), ["tu.sig"], tf("si"), ["tf.si"])
+        act(row("srow"), ["srow"], T.ramp[:].indirect(tu("sig")), ["ramp", "tu.sig"])
+        act(row("brow"), ["brow"], row("srow").indirect(tu("b")), ["srow", "tu.b"])
+        latch(row("brow"), "brow", row("c3"), "c3")
+        tabs("c3", tu("b"), ["tu.b"], 2)
+        for b in range(4):
+            act(row("r2%d" % b), ["r2%d" % b], T.pa[:, 512 * b:512 * b + C], ["pa%d" % b], 0.43, scale=0.015625)
+        for b in range(4):
+            tt(T.xt[:, b:4 * C:4], ["xt%d" % b], row("r2%d" % b).indirect(tu("b")), row("fh%d" % b), A.add, ["r2%d" % b, "fh%d" % b, "tu.b"], GAT)
+        quant("xt", ["xt0", "xt1", "xt2", "xt3"], C, "qx%d" % (r + 1))
+        if last:
+            break
+        ts(tf("t2x"), ["tf.t2x"], tf("t"), -2.0, None, A.mult, None, ["tf.t"])
+        tt(tf("dfm"), ["tf.dfm"], tf("dfm"), tf("t2x"), A.add, ["tf.dfm", "tf.t2x"])
+        frow()
+        levels()
+        state_made(r + 1)
         if r == 0:
-            op("v", lambda: g.vector.tensor_copy(row("brow").indirect(tu("tab0")), T.ramp[:, 0:C]), ["ramp", "tu.tab0"], ["brow"])
-        else:
-            act(row("srow"), ["srow"], T.ramp[:].indirect(tu("sig")), ["ramp", "tu.sig"])
-            act(row("brow"), ["brow"], row("srow").indirect(tu("b")), ["srow", "tu.b"])
-        for b in range(4):
-            act(row("r2%d" % b), ["r2%d" % b], T.pa[:, 512 * b:512 * b + C], ["pa%d" % b], func=AF.Copy, scale=0.015625)
-        if not last:
-            ts(tf("t"), ["tf.t"], tf("t"), -2.0, None, A.mult, None, ["tf.t"])
-            lev_key(0)
-            lev_km(0)
-            tt(tf("dfm"), ["tf.dfm"], tf("dfm"), tf("t"), A.add, ["tf.dfm", "tf.t"])
-        latch("brow", "cb")
-        tabs("cb", tu("b"), ["tu.b"], 2)
-        if not last:
-            lev_tab(0)
-        for b in range(4):
-            tt(T.xt[:, b:4 * C:4], ["xt%d" % b], row("r2%d" % b).indirect(tu("b")), row("fh%d" % b), A.add, ["r2%d" % b, "fh%d" % b, "tu.b"])
-        qn = "qx%d" % (r + 1)
-        if not last:
-            lev_row(1)
-        quant("xt", ["xt0", "xt1", "xt2", "xt3"], C, qn)
-        if not last:
-            sendx(r + 1)
-            scores(r + 1)
-            lev_key(1)
-            lev_tab(1)
-            lev_km(1)
-            for k in range(2, 9):
-                if k == 4:
-                    act(row("sr"), ["sr"], T.pb[:, 0:C], ["pb0"])
-                level(k)
-            if r == 0:
-                quant("vin", ["vin"], 128, "qv")
-            finish(r + 1)
+            quant("vin", ["vin"], 128, "qv")
+        finish(r + 1)
     def store(eng, out, src, keys):
-        op(eng, lambda: Q[eng].dma_start(out, src), keys, [], sem="outs", inc=16)
-    mm("pb", 0, "qv", 0, "qx3")
+        op(eng, lambda: Q[eng].dma_start(out, src), keys, [], 0.07, sem="outs", inc=16, lat=2.0)
+    act(row("nlr"), ["nlr"], T.ramp[:].indirect(tu("tab0")), ["ramp", "tu.tab0"], bias=224.0)
     store("y", T.nl[:], T.nlr[0:128:16, :], ["nlr"])
+    mm("pb", 0, "qv", 0, "qx3")
     store("y", T.oc[:], T.qx3[:, 0:C].bitcast(dt.uint8), ["qx3"])
-    act(row("ysb"), ["ysb"], T.pb[:, 0:C], ["pb0"])
+    act(row("ysb"), ["ysb"], T.pb[:, 0:C], ["pb0"], 0.43)
     for k in range(4):
         store("y", T.osc[4 * k:4 * k + 4, :], T.qx3s[32 * k:32 * k + 4, 0:C], ["qx3s"])
     store("s", T.y[:], row("ysb"), ["ysb"])
+
+    n = len(prog)
+    deps, kids = [set() for _ in range(n)], [[] for _ in range(n)]
+    lw, rd = {}, {}
+    for i, p in enumerate(prog):
+        for k in p["r"]:
+            if k in lw:
+                deps[i].add(lw[k])
+        for k in p["w"]:
+            if k in lw:
+                deps[i].add(lw[k])
+            deps[i].update(rd.get(k, []))
+        for k in p["r"]:
+            rd.setdefault(k, []).append(i)
+        for k in p["w"]:
+            lw[k], rd[k] = i, []
+        deps[i].discard(i)
+        for d in deps[i]:
+            kids[d].append(i)
+    prio = [0.0] * n
+    for i in range(n - 1, -1, -1):
+        prio[i] = prog[i]["c"] + prog[i]["lat"] + max([prio[k] + WAKE for k in kids[i]] + [0.0])
+    done, left, tq, order = {}, [len(d) for d in deps], {e: 0.0 for e in Q}, []
+    ready = {e: [] for e in Q}
+    for i in range(n):
+        if not left[i]:
+            ready[prog[i]["eng"]].append((0.0, i))
+    while len(order) < n:
+        pick = None
+        for e in Q:
+            if not ready[e]:
+                continue
+            t0 = max(tq[e], min(a for a, i in ready[e]))
+            a, i = max((x for x in ready[e] if x[0] <= t0 + 1e-9), key=lambda x: (prio[x[1]], -x[1]))
+            if pick is None or t0 < pick[0]:
+                pick = (t0, e, a, i)
+        t0, e, a, i = pick
+        ready[e].remove((a, i))
+        order.append(i)
+        tq[e] = t0 + prog[i]["c"]
+        done[i] = tq[e] + prog[i]["lat"] + WAKE
+        for k in kids[i]:
+            left[k] -= 1
+            if not left[k]:
+                ready[prog[k]["eng"]].append((max(done[d] for d in deps[k]), k))
+
+    cnt = {s: 0 for s in SEMAPHORES}
+    known = {e: {} for e in Q}
+    clock, lastw, readers = {}, {}, {}
+
+    def need(eng, ds):
+        best = {}
+        for s, v in ds:
+            best[s] = max(best.get(s, 0), v)
+        own = CS.get(eng)
+        for s in sorted(best, key=lambda x: (x == own, x)):
+            if known[eng].get(s, 0) >= best[s]:
+                continue
+            Q[eng].wait_ge(T.sem[s], best[s])
+            for x, y in clock[(s, best[s])].items():
+                known[eng][x] = max(known[eng].get(x, 0), y)
+
+    landed = {"aq%d" % i: 2 for i in range(3)}
+    for i in order:
+        p = prog[i]
+        ds = []
+        for k in p["r"]:
+            if k in lastw:
+                ds.append(lastw[k])
+        if p["remote"]:
+            need("g", ds)
+            p["fn"]()
+            sem, m = p["remote"]
+            cnt["snt"] += m
+            cnt[sem] += m
+            me = (sem, m * landed.get(sem, 1))
+            clock[me] = {sem: me[1]}
+            lastw[p["w"][0]] = me
+            continue
+        for k in p["w"]:
+            if k in lastw:
+                ds.append(lastw[k])
+            ds += readers.get(k, [])
+        need(p["eng"], ds)
+        s = p["sem"] or CS[p["eng"]]
+        cnt[s] += p["inc"]
+        p["fn"]().then_inc(T.sem[s], p["inc"])
+        me = (s, cnt[s])
+        clock[me] = dict(known[p["eng"]])
+        clock[me][s] = cnt[s]
+        for k in p["r"]:
+            readers.setdefault(k, []).append(me)
+        for k in p["w"]:
+            lastw[k] = me
+            readers[k] = []
     for s in SEMAPHORES:
         if cnt[s] and known["g"].get(s, 0) < cnt[s]:
             g.wait_ge(T.sem[s], cnt[s])

@@ -3,22 +3,26 @@ from concourse.mybir import dt, AluOpType, ActivationFunctionType
 C = 448
 TW = 28
 STEP = [1, 2, 3]
+NP = 1
 SCRATCH = {}
 
 
 def _decl():
     f32, bf, f16 = "float32", "bfloat16", "float16"
-    for n in ["k0", "k0m", "kc", "cpr", "ka", "kb", "kma", "kmb", "lraw", "ln", "cs", "sr", "sa", "cand", "mu", "nu", "sgn", "ck", "lck", "nlr", "ysb"]:
+    for n in ["k0", "k0m", "kc", "cpr", "ka", "kb", "kma", "kmb", "kd", "yk", "yr", "cs", "sr", "sa", "cand", "mu", "nu", "sgn", "ck", "lck", "nlr", "ysb"]:
         SCRATCH[n] = ("sbuf", [128, C], f32)
     for n in ["cp", "rst", "pm", "cm"]:
         SCRATCH[n] = ("sbuf", [128, C + 8], f32)
-    for n in ["eq", "lrow", "plr", "tplr", "tcsr", "tlenr", "trow", "sw", "csr", "lnr", "srow", "brow", "lc", "fmr"]:
+    for n in ["eq", "lrow", "plr", "tplr", "tcsr", "tlenr", "trow", "sw", "srow", "brow", "lc", "fmr"]:
         SCRATCH[n] = ("sbuf", [128, C], bf)
     SCRATCH["ar"] = ("sbuf", [128, C + 16], bf)
+    for b in range(4 - NP, 4):
+        SCRATCH["pp%d" % b] = ("sbuf", [128, C], f32)
     SCRATCH["ramp"] = ("sbuf", [128, C + 16], bf)
     SCRATCH["ro"] = ("sbuf", [128, 9 * C], bf)
     SCRATCH["cc"] = ("sbuf", [128, 6 * C], f16)
-    SCRATCH["c2s"] = ("sbuf", [128, 2 * C], f16)
+    SCRATCH["drow"] = SCRATCH["plg"] = ("sbuf", [128, C], bf)
+    SCRATCH["cl"] = SCRATCH["nsgn"] = ("sbuf", [128, C], f32)
     SCRATCH["c4s"] = ("sbuf", [128, 4 * C], f16)
     SCRATCH["gr"] = ("sbuf", [128, 4 * C], bf)
     for b in range(4):
@@ -34,7 +38,7 @@ def _decl():
         SCRATCH[n] = ("sbuf", [128, w], "float8_e4m3fn_x4")
         SCRATCH[n + "s"] = ("sbuf", [128, w], "uint8")
     for n, w, t in [("fl_s", TW, "int32"), ("ml_s", TW, "int32"), ("pq", TW, "int32"), ("pqm", TW, "int32"), ("ofq", TW, "uint16"), ("ofi", 8, "int32"), ("ofu", 8, "uint16"),
-                    ("col", 8, f32), ("tf", TW * 36, f32), ("ti", TW * 4, "int32"), ("tu", TW * 16, "uint16"), ("t16", 16, bf), ("la16", 16, bf), ("lb16", 16, bf), ("lc16", 16, bf)]:
+                    ("col", 12, f32), ("tf", TW * 50, f32), ("ti", TW * 4, "int32"), ("tu", TW * 20, "uint16"), ("t16", 16, bf), ("la16", 16, bf), ("lb16", 16, bf), ("lc16", 16, bf)]:
         SCRATCH[n] = ("sbuf", [128, w], t)
     for i in range(3):
         SCRATCH["sp%d" % i] = ("sbuf", [128, 3 * TW], "uint16")
@@ -48,12 +52,13 @@ def _decl():
 _decl()
 LOADS = ["dfl", "dml", "dx", "du", "dv", "dwc", "dws"]
 SEMAPHORES = ["cv", "cs_", "ct", "cg", "snt", "outs"] + LOADS + ["%s%d" % (n, i) for n in ("aq", "al", "aa") for i in range(3)]
-TF = {n: i for i, n in enumerate(["jt", "f", "m", "mj", "fm", "dfm", "t", "t2x", "ln", "cs", "pl", "g0", "g1", "g2", "g3", "i0", "ng", "t1", "p0", "pi", "u", "inv", "bq",
-                                  "t2", "tp", "sw", "sg", "si", "sn", "e1", "wr", "wl", "pb"])}
-TU = {n: i for i, n in enumerate(["tab%d" % k for k in range(9)] + ["m", "root", "l", "tp", "T", "sig", "b"])}
+TF = {n: i for i, n in enumerate(["jt", "f", "m", "hf", "fm", "cf", "hm", "cm", "ln", "cs", "pl", "g0", "g1", "g2", "g3", "i0", "ng", "t1", "p0", "pi", "u", "inv", "bq",
+                                  "t2", "tp", "sw", "sg", "si", "sn", "e1", "wr", "wl", "pb", "kmd", "lx", "ple", "ple2", "c2", "pre0", "pre", "vv", "vp", "w", "l3"])}
+TU = {n: i for i, n in enumerate(["tab%d" % k for k in range(9)] + ["m", "root", "l", "tp", "T", "sig", "b"] + ["end"])}
 TI = {"k": 0, "root": 1, "d": 2, "n": 3}
+BIAS = {"pp": 1.0, "lq": -2.0, "qz": 4.0, "tu.sig": 1.0}
 H, HW = 192, 12
-GAT, HALF, TINY, WAKE = 0.70, 0.38, 0.12, 0.06
+GAT, HALF, TINY, WAKE = 0.62, 0.32, 0.06, 0.15
 
 
 def rank_program(g, core, T, topo):
@@ -132,12 +137,13 @@ def rank_program(g, core, T, topo):
     iota(T.pq[:], ["pq"], [[0, TW]], 0, 1, TW, False)
     iota(T.t16[:], ["t16"], [[1, 16]], 0, 0, 16)
     iota(T.ramp[:], ["ramp"], [[1, C + 16]], -224, 0, C + 16)
-    iota(row("k0"), ["k0"], [[512, C]], 0, 0, C)
-    iota(row("k0m"), ["k0m"], [[512, C]], -1, 0, C)
+    iota(row("k0"), ["k0"], [[1024, C]], 0, 0, C)
+    iota(row("k0m"), ["k0m"], [[1024, C]], -1, 0, C)
     iota(tf("jt"), ["jt0"], [[16, TW]], 0, 0, TW)
     iota(T.ofi[:], ["ofi"], [[16, 8]], 0, 0, 8, False)
     iota(row("cpr"), ["cpr"], [[-1, C]], 449, 0, C)
-    iota(row("kc"), ["kc"], [[512, C]], -512, 0, C)
+    iota(row("kd"), ["kd"], [[1024, C]], -1536, 0, C)
+    iota(row("kc"), ["kc"], [[1024, C]], -512, 0, C)
     ts(T.pqm[:], ["pqm"], T.pq[:], 15, None, A.bitwise_and, None, ["pq"])
     cp(cl(0), ["col0"], T.pqm[:, 0:1], ["pqm"])
     cp(T.ofq[:], ["ofq"], T.pqm[:], ["pqm"])
@@ -148,18 +154,20 @@ def rank_program(g, core, T, topo):
     ts(T.lb16[:], ["lb16"], T.t16[:], 15.0, -1024.0, A.is_equal, A.mult, ["t16"])
     tt(T.lc16[:], ["lc16"], T.la16[:], T.lb16[:], A.add, ["la16", "lb16"])
     act(row("lc"), ["lc"], T.lc16[:].indirect(T.ofq[:]), ["lc16", "ofq"])
-    act(row("lck"), ["lck"], row("lc"), ["lc"], 0.43, scale=512.0)
+    act(row("lck"), ["lck"], row("lc"), ["lc"], 0.43, scale=1024.0)
     ts(cl(1), ["col1"], cl(0), 0.0, 1024.0, A.is_equal, A.mult, ["col0"])
     ts(cl(1), ["col1"], cl(1), -512.0, None, A.add, None, ["col1"])
     ts(cl(2), ["col2"], cl(1), 224.0, None, A.add, None, ["col1"])
-    ts(cl(3), ["col3"], cl(1), 512.0, 511.0, A.mult, A.add, ["col1"])
-    ts(cl(6), ["col6"], cl(1), 511.0 / 512 - 0.499, None, A.add, None, ["col1"])
+    ts(cl(3), ["col3"], cl(1), 1024.0, 511.0, A.mult, A.add, ["col1"])
+    ts(cl(8), ["col8"], cl(1), 1024.0, 512.0, A.mult, A.add, ["col1"])
+    ts(cl(7), ["col7"], cl(1), -2.0, 1.0, A.mult, A.add, ["col1"])
+    ts(cl(6), ["col6"], cl(1), 511.0 / 1024 + 0.01, None, A.add, None, ["col1"])
     ts(cl(4), ["col4"], cl(1), -1.0, 449.0, A.mult, A.add, ["col1"])
     ts(cl(5), ["col5"], cl(1), -1.0, 224.0, A.mult, A.add, ["col1"])
     for n in ["cp", "rst", "pm", "cm"]:
         op("v", lambda n=n: g.vector.memset(T[n][:, 0:1], 0.0), [], [n + "0"])
     op("v", lambda: g.vector.memset(T.ar[:, 0:1], 0.0), [], ["ar0"])
-    op("v", lambda: g.vector.memset(T.et[:], 1.0), [], ["et1"], 0.5)
+    op("v", lambda: g.vector.memset(T.et[:], 0.5), [], ["et1"], 0.5)
     op("g", lambda: g.affine_select(T.et[:], T.et[:], [[-1, 4], [1, 512]], A.is_equal, 0.0, 0, -4), ["et1"], ["et"], 3.6)
     cp(tu("tab0"), ["tu.tab0"], T.fl_s[:], ["fl_s"])
 
@@ -199,24 +207,33 @@ def rank_program(g, core, T, topo):
 
     def finish(r):
         sp, sl = "sp%d" % r, "sl%d" % r
-        tt(row("lraw"), ["lraw"], row(KF).indirect(tu("tab0")), row("kc"), A.subtract, [KF, "tu.tab0", "kc"], GAT)
-        act(row("ln"), ["ln"], row("lraw"), ["lraw"], 0.43, func=AF.Relu)
-        scan(row("ck"), ["ck"], row(KF), row("lck"), -524288.0, A.max, A.add, [KF, "lck"])
+        tt(row("yk"), ["yk"], row(KF).indirect(tu("tab0")), row("kc"), A.max, [KF, "tu.tab0", "kc"], GAT)
+        scan(row("ck"), ["ck"], row(KF), row("lck"), -1048576.0, A.max, A.add, [KF, "lck"])
+        ts(tu("root"), ["tu.root"], T.ck[:, 15:C:16], 2.0 ** -10, cl(6), A.mult, A.add, ["ck", "col6"])
         ts(ti("k"), ["ti.k"], T.ck[:, 15:C:16], cl(3), None, A.add, None, ["ck", "col3"])
-        ts(ti("root"), ["ti.root"], T.ck[:, 15:C:16], 2.0 ** -9, cl(6), A.mult, A.add, ["ck", "col6"])
-        cp(tu("root"), ["tu.root"], ti("root"), ["ti.root"])
         ts(ti("d"), ["ti.d"], ti("k"), 511, None, A.bitwise_and, None, ["ti.k"])
-        act(row("lnr"), ["lnr"], row("lraw").indirect(tu("root")), ["lraw", "tu.root"], bias=-224.0)
-        scan(row("cs"), ["cs"], row("ln"), row("ln"), 0.0, A.add, A.max, ["ln"])
-        ts(row("csr"), ["csr"], row("cs").indirect(tu("root")), -224.0, None, A.add, None, ["cs", "tu.root"], GAT)
-        latch(row("lnr"), "lnr", T.c2s[:, 0:C], "c2a")
-        latch(row("csr"), "csr", T.c2s[:, C:2 * C], "c2b")
-        ts(T.tf[:, TW * TF["ln"]:TW * (TF["ln"] + 2)], ["tf.lc"], T.c2s[:, 15:2 * C:16], cl(2), None, A.add, None, ["c2a", "c2b", "col2"])
-        tt(tf("pl"), ["tf.pl"], tf("cs"), ti("d"), A.subtract, ["tf.lc", "ti.d"])
-        cp(T[sp][:, 0:TW], [sp + "a"], tf("pl"), ["tf.pl"])
-        op("v", lambda: g.vector.tensor_copy(win1("cp").indirect(T[sp][:, 0:TW]), row("cpr")), ["cpr", sp + "a", "cp0"], ["cp"], 1.5)
-        cp(T[sp][:, TW:3 * TW], [sp + "b"], T.tf[:, TW * TF["ln"]:TW * (TF["ln"] + 2)], ["tf.lc"])
-        send(r, "lp%d" % r, sp, [sp + "a", sp + "b"], "al%d" % r, w=3 * TW)
+        cp(T[sp][:, 2 * TW:3 * TW], [sp + "d"], ti("d"), ["ti.d"])
+        tt(tf("kmd"), ["tf.kmd"], ti("k"), ti("d"), A.subtract, ["ti.k", "ti.d"])
+        act(row("yr"), ["yr"], row("yk").indirect(tu("root")), ["yk", "tu.root"])
+        act(row("drow"), ["drow"], T.ramp[:].indirect(T[sp][:, 2 * TW:3 * TW]), ["ramp", sp + "d"])
+        scan(row("cs"), ["cs"], row("yk"), row("kd"), -1024.0 - 224.0 - 511.0, A.add, A.subtract, ["yk", "kd"])
+        tt(row("plg"), ["plg"], row("cs").indirect(tu("root")), row(KF), A.subtract, ["cs", "tu.root", KF], GAT)
+        latch(row("plg"), "plg", row("c2"), "c2")
+        tabs("c2", T[sp][:, 0:TW], [sp + "a"], 2)
+        op("v", lambda: g.vector.tensor_copy(win1("cp").indirect(T[sp][:, 0:TW]), row("cpr")), ["cpr", sp + "a", "cp0"], ["cp"], 1.4)
+        scan(row("cl"), ["cl"], row("yr"), row("lck"), -1048576.0, A.max, A.add, ["yr", "lck"])
+        ts(tf("lx"), ["tf.lx"], T["cl"][:, 15:C:16], cl(8), None, A.add, None, ["cl", "col8"])
+        tt(tf("ln"), ["tf.ln"], tf("lx"), tf("kmd"), A.subtract, ["tf.lx", "tf.kmd"])
+        cp(T[sp][:, TW:2 * TW], [sp + "b"], tf("ln"), ["tf.ln"])
+        tabs("c2", tf("pl"), ["tf.pl"], 2)
+        ts(tf("ple"), ["tf.ple"], tf("pl"), cl(2), None, A.subtract, None, ["tf.pl", "col2"])
+        ts(tf("ple2"), ["tf.ple2"], tf("ple"), cl(2), None, A.subtract, None, ["tf.ple", "col2"])
+        tt(tf("cs"), ["tf.cs"], tf("pl"), ti("d"), A.add, ["tf.pl", "ti.d"])
+        cp(tu("end"), ["tu.end"], tf("cs"), ["tf.cs"])
+        ts(tf("c2"), ["tf.c2"], tf("cf"), -2.0, None, A.mult, None, ["tf.cf"])
+        ts(tf("pre0"), ["tf.pre0"], tf("cf"), cl(7), None, A.mult, None, ["tf.cf", "col7"])
+        tt(tf("pre"), ["tf.pre"], tf("pre0"), tf("hf"), A.add, ["tf.pre0", "tf.hf"])
+        send(r, "lp%d" % r, sp, [sp + "a", sp + "b", sp + "d"], "al%d" % r, w=3 * TW)
         latch(row1("cp"), "cp", row("c4"), "c4")
         tabm("c4", T[sl][:], [sl], 4)
         send(r, "la%d" % r, sl, [sl], "aa%d" % r, w=TW)
@@ -232,7 +249,7 @@ def rank_program(g, core, T, topo):
         send(r, "lq%d" % r, "qx%d" % r, ["qx%d" % r], "aq%d" % r, code=True)
         send(r, "lq%ds" % r, "qx%ds" % r, ["qx%ds" % r], "aq%d" % r)
         mm("pb", 0, "qur", 0, "qx%d" % r)
-        act(row("sr"), ["sr"], T.pb[:, 0:C], ["pb0"], 0.43)
+        act(row("sr"), ["sr"], T.pb[:, 0:C], ["pb0", "ro8"], 0.43)
         for b in range(4):
             mm("pa", b, "qe", 128 * b, "qx%d" % r)
         for b in range(4):
@@ -243,16 +260,20 @@ def rank_program(g, core, T, topo):
     cp(tu("m"), ["tu.m"], T.ml_s[:], ["ml_s"])
     cp(tf("f"), ["tf.f"], T.fl_s[:], ["fl_s"])
     cp(tf("m"), ["tf.m"], T.ml_s[:], ["ml_s"])
-    act(row("fmr"), ["fmr"], row("ro0").indirect(tu("m")), ["ro0", "tu.m"])
+    act(row("fmr"), ["fmr"], row("ro0").indirect(tu("m")), ["ro0", "tu.m", "ro8"])
     latch(row("fmr"), "fmr", row("c2"), "c2")
     tabs("c2", tf("fm"), ["tf.fm"], 2)
-    tt(tf("dfm"), ["tf.dfm"], tf("fm"), tf("f"), A.subtract, ["tf.fm", "tf.f"])
+    tt(tf("hf"), ["tf.hf"], tf("fm"), tf("f"), A.add, ["tf.fm", "tf.f"])
+    ts(tf("hf"), ["tf.hf"], tf("hf"), 0.5, None, A.mult, None, ["tf.hf"])
+    tt(tf("cf"), ["tf.cf"], tf("f"), tf("hf"), A.subtract, ["tf.f", "tf.hf"])
     ts(tf("jt"), ["tf.jt"], tf("jt"), cl(0), None, A.add, None, ["jt0", "col0"])
-    tt(tf("mj"), ["tf.mj"], tf("m"), tf("jt"), A.subtract, ["tf.m", "tf.jt"])
-    ts(tf("sn"), ["tf.sn"], tf("mj"), 0.0, 2.0, A.is_gt, A.mult, ["tf.mj"])
+    tt(tf("hm"), ["tf.hm"], tf("m"), tf("jt"), A.add, ["tf.m", "tf.jt"])
+    ts(tf("hm"), ["tf.hm"], tf("hm"), 0.5, None, A.mult, None, ["tf.hm"])
+    tt(tf("cm"), ["tf.cm"], tf("jt"), tf("hm"), A.subtract, ["tf.jt", "tf.hm"])
+    ts(tf("sn"), ["tf.sn"], tf("cm"), 0.0, 2.0, A.is_lt, A.mult, ["tf.cm"])
     ts(tu("sig"), ["tu.sig"], tf("sn"), 223.0, None, A.add, None, ["tf.sn"])
-    act(row("sgn"), ["sgn"], T.ramp[:].indirect(tu("sig")), ["ramp", "tu.sig"])
-    quant("xin", ["xin"], C, "qx0")
+    act(row("sgn"), ["sgn"], T.ramp[:].indirect(tu("sig")), ["ramp", "tu.sig", "ro8"])
+    quant("xin", ["xin", "tu.tab2"], C, "qx0")
     quant("uin", ["uin"], 128, "qu")
     cp(T.ofu[:], ["ofu"], T.ofi[:], ["ofi"])
     op("v", lambda: g.vector.tensor_copy(T.qur[:, 0:128].bitcast(dt.uint32), T.qu[:, 0:128].bitcast(dt.uint32).indirect(T.ofu[:, 0:8])), ["qu", "ofu"], ["qur"], 0.27)
@@ -260,9 +281,10 @@ def rank_program(g, core, T, topo):
     quant("et", ["et"], 512, "qe")
     state_made(0)
     finish(0)
+    act(row("nsgn"), ["nsgn"], row("sgn"), ["sgn", "yr"], 0.43, scale=-1.0)
     ts(tf("e1"), ["tf.e1"], ti("d"), 1.0, None, A.add, None, ["ti.d"])
-    tt(tf("wr"), ["tf.wr"], tf("e1"), tf("ln"), A.is_equal, ["tf.e1", "tf.lc"])
-    tt(tf("wl"), ["tf.wl"], tf("wr"), tf("ln"), A.mult, ["tf.wr", "tf.lc"])
+    tt(tf("wr"), ["tf.wr"], tf("e1"), tf("ln"), A.is_equal, ["tf.e1", "tf.ln"])
+    tt(tf("wl"), ["tf.wl"], tf("wr"), tf("ln"), A.mult, ["tf.wr", "tf.ln"])
     tt(tf("pb"), ["tf.pb"], tf("pl"), tf("wl"), A.add, ["tf.pl", "tf.wl"])
     ts(tu("b"), ["tu.b"], tf("pb"), -1.0, None, A.add, None, ["tf.pb"])
     act(row("brow"), ["brow"], win1("cp").indirect(tu("b")), ["cp", "tu.b"], scale=-1.0, bias=225.0)
@@ -270,24 +292,22 @@ def rank_program(g, core, T, topo):
     tabs("c3", tu("b"), ["tu.b"], 2)
 
     grs = lambda i: T.gr[:, C * i:C * i + C]
-    c4s = lambda i: T.c4s[:, C * i:C * i + C]
     for r in range(3):
         sl, lp, la, sp = "sl%d" % r, "lp%d" % r, "la%d" % r, "sp%d" % r
         last = r == 2
-        end = T[sp][:, 2 * TW:3 * TW]
-        act(row1("rst"), ["rst"], row("ln").indirect(T[sl][:]), ["ln", sl, "rst0"], scale=-float(2 ** 90))
+        act(row1("rst"), ["rst"], row("drow").indirect(T[sl][:]), ["drow", sl, "rst0"], scale=float(2 ** 90), bias=223.5 * float(2 ** 90))
         cp(row("sa"), ["sa"], row("sr").indirect(T[sl][:]), ["sr", sl], GAT)
-        scan(row1("pm"), ["pm"], row("rst"), row("sa"), -float(2 ** 90), A.add, A.max, ["rst", "rst0", "sa", "pm0"])
-        tt(row("eq"), ["eq"], win1("pm").indirect(end), row("sr"), A.is_equal, ["pm", sp + "b", "sr"], GAT)
+        scan(row1("pm"), ["pm"], row("rst"), row("sa"), -float(2 ** 90), A.min, A.max, ["rst", "rst0", "sa", "pm0"])
+        tt(row("eq"), ["eq"], win1("pm").indirect(tu("end")), row("sr"), A.is_equal, ["pm", "tu.end", "sr"], GAT)
         tt(row("cand"), ["cand"], row("eq").indirect(T[sl][:]), row1("cp"), A.mult, ["eq", sl, "cp"], GAT)
-        scan(row1("cm"), ["cm"], row("rst"), row("cand"), 0.0, A.add, A.max, ["rst", "cand", "cm0"])
-        act(T.lrow[:, 0:H], ["lrowa"], win1("cm").indirect(T[sp][:, 2 * TW:2 * TW + HW]), ["cm", sp + "b"], HALF, bias=-225.0)
-        ts(T.lrow[:, H:C], ["lrowb"], win1("cm").indirect(T[sp][:, 2 * TW + HW:3 * TW]), -225.0, None, A.add, None, ["cm", sp + "b"], HALF)
+        scan(row1("cm"), ["cm"], row("rst"), row("cand"), 0.0, A.min, A.max, ["rst", "cand", "cm0"])
+        act(T.lrow[:, 0:H], ["lrowa"], win1("cm").indirect(tu("end", 0, HW)), ["cm", "tu.end"], HALF, bias=-225.0)
+        ts(T.lrow[:, H:C], ["lrowb"], win1("cm").indirect(tu("end", HW)), -225.0, None, A.add, None, ["cm", "tu.end"], HALF)
         latch(row("lrow"), ["lrowa", "lrowb"], row("c5"), "c5")
         tabm("c5", tu("l"), ["tu.l"], 5)
         act(row("plr"), ["plr"], T.ramp[:].indirect(T[sp][:, 0:TW]), ["ramp", sp + "a"])
         for b in range(4):
-            act(row("fh%d" % b), ["fh%d" % b], T.pa[:, 512 * b:512 * b + C], ["pa%d" % b], 0.43, scale=0.5)
+            act(row("fh%d" % b), ["fh%d" % b], T.pa[:, 512 * b:512 * b + C], ["pa%d" % b, "yr"], 0.43)
         act(row("tcsr"), ["tcsr"], T.ramp[:].indirect(T[lp][:, 2 * TW:3 * TW]), ["ramp", lp])
         act(row("tlenr"), ["tlenr"], T.ramp[:].indirect(T[lp][:, TW:2 * TW]), ["ramp", lp])
         act(row("tplr"), ["tplr"], T.ramp[:].indirect(T[lp][:, 0:TW]), ["ramp", lp])
@@ -297,20 +317,23 @@ def rank_program(g, core, T, topo):
         act(grs(0), ["gr0"], row("tplr").indirect(tu("l")), ["tplr", "tu.l"])
         act(row1("ar"), ["ar"], T.ramp[:].indirect(T[la][:]), ["ramp", la, "ar0"])
         for i in (3, 1, 2, 0):
-            latch(grs(i), "gr%d" % i, c4s(i), "c4s%d" % i)
-        ts(T.tf[:, TW * TF["g0"]:TW * (TF["g0"] + 4)], ["tf.g"], T.c4s[:, 15:4 * C:16], cl(2), None, A.add, None, ["c4s0", "c4s1", "c4s2", "c4s3", "col2"], 0.15)
+            latch(grs(i), "gr%d" % i, T.c4s[:, C * i:C * i + C], "c4s%d" % i)
+        x = lambda i: T.c4s[:, C * i + 15:C * i + C:16]
         for b in range(4):
-            act(row("ft%d" % b), ["ft%d" % b], T.pb[:, 512 * b:512 * b + C], ["pb%d" % b], 0.43, scale=0.5)
-        op("v", lambda: g.vector.reciprocal(tf("inv"), tf("g3")), ["tf.g"], ["tf.inv"], 0.35)
-        tt(tf("i0"), ["tf.i0"], tf("pl"), tf("g1"), A.subtract, ["tf.g", "tf.pl"])
-        ts(tf("ng"), ["tf.ng"], tf("i0"), 0.0, None, A.is_lt, None, ["tf.i0"])
-        tt(tf("p0"), ["tf.p0"], tf("g0"), tf("i0"), A.add, ["tf.g", "tf.i0"])
-        tt(tf("t1"), ["tf.t1"], tf("ng"), tf("ln"), A.mult, ["tf.ng", "tf.lc"])
+            act(row("ft%d" % b), ["ft%d" % b], T.pb[:, 512 * b:512 * b + C], ["pb%d" % b, "gr0"], 0.43)
+        ts(tf("l3"), ["tf.l3"], x(3), cl(2), None, A.add, None, ["c4s3", "col2"])
+        tt(tf("ng"), ["tf.ng"], tf("ple"), x(1), A.is_lt, ["c4s1", "tf.ple"])
+        tt(tf("vv"), ["tf.vv"], tf("ple2"), x(1), A.subtract, ["c4s1", "tf.ple2"])
+        tt(tf("vp"), ["tf.vp"], tf("pl"), x(1), A.subtract, ["c4s1", "tf.pl"])
+        op("v", lambda: g.vector.reciprocal(tf("inv"), tf("l3")), ["tf.l3"], ["tf.inv"], 0.33)
+        tt(tf("t1"), ["tf.t1"], tf("ng"), tf("ln"), A.mult, ["tf.ng", "tf.ln"])
+        tt(tf("w"), ["tf.w"], x(2), tf("vv"), A.subtract, ["c4s2", "tf.vv"])
+        tt(tf("u"), ["tf.u"], tf("w"), tf("t1"), A.subtract, ["tf.w", "tf.t1"])
+        tt(tf("p0"), ["tf.p0"], x(0), tf("vp"), A.add, ["c4s0", "tf.vp"])
         tt(tf("pi"), ["tf.pi"], tf("p0"), tf("t1"), A.add, ["tf.p0", "tf.t1"])
-        tt(tf("u"), ["tf.u"], tf("g2"), tf("pi"), A.subtract, ["tf.pi", "tf.g"])
         tt(tf("bq"), ["tf.bq"], tf("u"), tf("inv"), A.mult, ["tf.u", "tf.inv"])
         ts(ti("n"), ["ti.n"], tf("bq"), -0.4989, None, A.add, None, ["tf.bq"])
-        tt(tf("t2"), ["tf.t2"], ti("n"), tf("g3"), A.mult, ["ti.n", "tf.g"])
+        tt(tf("t2"), ["tf.t2"], ti("n"), tf("l3"), A.mult, ["ti.n", "tf.l3"])
         tt(tf("tp"), ["tf.tp"], tf("pi"), tf("t2"), A.add, ["tf.pi", "tf.t2"])
         cp(tu("tp"), ["tu.tp"], tf("tp"), ["tf.tp"])
         act(T.trow[:, 0:H], ["trowa"], win1("ar").indirect(tu("tp", 0, HW)), ["ar", "tu.tp"], HALF)
@@ -320,34 +343,37 @@ def rank_program(g, core, T, topo):
         tt(row("mu"), ["mu"], row("sr").indirect(tu("T")), row("sgn"), A.mult, ["sr", "tu.T", "sgn"], GAT)
         for b in range(4):
             act(row("fs%d" % b), ["fs%d" % b], row("ft%d" % b).indirect(tu("T")), ["ft%d" % b, "tu.T"])
-        act(row("nu"), ["nu"], row("mu"), ["mu"], 0.43, scale=-1.0)
+        tt(row("nu"), ["nu"], row("sr").indirect(tu("T")), row("nsgn"), A.mult, ["sr", "tu.T", "nsgn"], GAT)
         tt(row("sw"), ["sw"], row("mu").indirect(tu("m")), row("nu"), A.is_lt, ["mu", "nu", "tu.m"], GAT)
         latch(row("sw"), "sw", row("c5"), "c5")
-        tabs("c5", tf("sw"), ["tf.sw"], 1)
-        tt(tf("t"), ["tf.t"], tf("sw"), tf("dfm"), A.mult, ["tf.sw", "tf.dfm"])
-        tt(tf("f"), ["tf.f"], tf("f"), tf("t"), A.add, ["tf.f", "tf.t"])
+        ts(tf("sw"), ["tf.sw"], sampled("c5"), -2.0, cl(7), A.mult, A.add, ["c5", "col7"])
+        tt(tf("si"), ["tf.si"], sampled("c5"), tf("c2"), A.mult, ["c5", "tf.c2"])
+        tt(tf("f"), ["tf.f"], tf("si"), tf("pre"), A.add, ["tf.si", "tf.pre"])
+        tt(tf("cf"), ["tf.cf"], tf("sw"), tf("cf"), A.mult, ["tf.sw", "tf.cf"])
         cp(tu("tab0"), ["tu.tab0"], tf("f"), ["tf.f"])
         for b in range(4):
             tt(T.zt[:, b:4 * C:4], ["zt%d" % b], row("fh%d" % b).indirect(tu("tab0")), row("fs%d" % b), A.add, ["fh%d" % b, "fs%d" % b, "tu.tab0"], GAT)
         quant("zt", ["zt0", "zt1", "zt2", "zt3"], C, "qz")
         for b in range(4):
-            mm("pa", b, "wq", 128 * b, "qz")
-        tt(tf("sg"), ["tf.sg"], tf("sw"), tf("mj"), A.mult, ["tf.sw", "tf.mj"])
-        tt(tf("si"), ["tf.si"], tf("sg"), tf("jt"), A.add, ["tf.sg", "tf.jt"])
+            mm("pb", b, "wq", 128 * b, "qz")
+        tt(tf("sg"), ["tf.sg"], tf("sw"), tf("cm"), A.mult, ["tf.sw", "tf.cm"])
+        tt(tf("si"), ["tf.si"], tf("sg"), tf("hm"), A.add, ["tf.sg", "tf.hm"])
         cp(tu("sig"), ["tu.sig"], tf("si"), ["tf.si"])
         act(row("srow"), ["srow"], T.ramp[:].indirect(tu("sig")), ["ramp", "tu.sig"])
         act(row("brow"), ["brow"], row("srow").indirect(tu("b")), ["srow", "tu.b"])
         latch(row("brow"), "brow", row("c3"), "c3")
         tabs("c3", tu("b"), ["tu.b"], 2)
         for b in range(4):
-            act(row("r2%d" % b), ["r2%d" % b], T.pa[:, 512 * b:512 * b + C], ["pa%d" % b], 0.43, scale=0.015625)
+            act(row("r2%d" % b), ["r2%d" % b], T.pb[:, 512 * b:512 * b + C], ["pb%d" % b], 0.43, scale=0.015625)
         for b in range(4):
+            if b >= 4 - NP and not last:
+                act(row("pp%d" % b), ["pp%d" % b], row("r2%d" % b).indirect(tu("b")), ["r2%d" % b, "tu.b"])
+                tt(T.xt[:, b:4 * C:4], ["xt%d" % b], row("pp%d" % b), T.pa[:, 512 * b:512 * b + C], A.add, ["pp%d" % b, "pa%d" % b], 0.43)
+                continue
             tt(T.xt[:, b:4 * C:4], ["xt%d" % b], row("r2%d" % b).indirect(tu("b")), row("fh%d" % b), A.add, ["r2%d" % b, "fh%d" % b, "tu.b"], GAT)
         quant("xt", ["xt0", "xt1", "xt2", "xt3"], C, "qx%d" % (r + 1))
         if last:
             break
-        ts(tf("t2x"), ["tf.t2x"], tf("t"), -2.0, None, A.mult, None, ["tf.t"])
-        tt(tf("dfm"), ["tf.dfm"], tf("dfm"), tf("t2x"), A.add, ["tf.dfm", "tf.t2x"])
         frow()
         levels()
         state_made(r + 1)
@@ -386,6 +412,8 @@ def rank_program(g, core, T, topo):
     prio = [0.0] * n
     for i in range(n - 1, -1, -1):
         prio[i] = prog[i]["c"] + prog[i]["lat"] + max([prio[k] + WAKE for k in kids[i]] + [0.0])
+    for i in range(n):
+        prio[i] += BIAS.get(prog[i]["w"][0].rstrip("0123456789") if prog[i]["w"] else "", 0.0)
     done, left, tq, order = {}, [len(d) for d in deps], {e: 0.0 for e in Q}, []
     ready = {e: [] for e in Q}
     for i in range(n):

from concourse.mybir import dt, AluOpType, ActivationFunctionType

C = 448
TW = 28
STEP = [1, 2, 3]
NP = 1
SCRATCH = {}


def _decl():
    f32, bf, f16 = "float32", "bfloat16", "float16"
    for n in ["k0", "k0m", "kc", "cpr", "ka", "kb", "kma", "kmb", "kd", "yk", "yr", "cs", "sr", "sa", "cand", "mu", "nu", "sgn", "ck", "lck", "nlr", "ysb"]:
        SCRATCH[n] = ("sbuf", [128, C], f32)
    for n in ["cp", "rst", "pm", "cm"]:
        SCRATCH[n] = ("sbuf", [128, C + 8], f32)
    for n in ["eq", "lrow", "plr", "tplr", "tcsr", "tlenr", "trow", "sw", "srow", "brow", "lc", "fmr"]:
        SCRATCH[n] = ("sbuf", [128, C], bf)
    SCRATCH["ar"] = ("sbuf", [128, C + 16], bf)
    for b in range(4 - NP, 4):
        SCRATCH["pp%d" % b] = ("sbuf", [128, C], f32)
    SCRATCH["ramp"] = ("sbuf", [128, C + 16], bf)
    SCRATCH["ro"] = ("sbuf", [128, 9 * C], bf)
    SCRATCH["cc"] = ("sbuf", [128, 6 * C], f16)
    SCRATCH["drow"] = SCRATCH["plg"] = ("sbuf", [128, C], bf)
    SCRATCH["cl"] = SCRATCH["nsgn"] = ("sbuf", [128, C], f32)
    SCRATCH["c4s"] = ("sbuf", [128, 4 * C], f16)
    SCRATCH["gr"] = ("sbuf", [128, 4 * C], bf)
    for b in range(4):
        for n in ["fh", "ft", "fs"]:
            SCRATCH[n + str(b)] = ("sbuf", [128, C], bf)
        SCRATCH["r2" + str(b)] = ("sbuf", [128, C], f32)
    for n in ["xin", "xt", "zt"]:
        SCRATCH[n] = ("sbuf", [128, 4 * C], bf)
    for n in ["uin", "vin"]:
        SCRATCH[n] = ("sbuf", [128, 512], bf)
    SCRATCH["et"] = ("sbuf", [128, 2048], bf)
    for n, w in [("wq", 512), ("qe", 512), ("qu", 128), ("qur", 128), ("qv", 128), ("qz", C)] + [("qx%d" % i, C) for i in range(4)] + [("lq%d" % i, C) for i in range(3)]:
        SCRATCH[n] = ("sbuf", [128, w], "float8_e4m3fn_x4")
        SCRATCH[n + "s"] = ("sbuf", [128, w], "uint8")
    for n, w, t in [("fl_s", TW, "int32"), ("ml_s", TW, "int32"), ("pq", TW, "int32"), ("pqm", TW, "int32"), ("ofq", TW, "uint16"), ("ofi", 8, "int32"), ("ofu", 8, "uint16"),
                    ("col", 12, f32), ("tf", TW * 50, f32), ("ti", TW * 4, "int32"), ("tu", TW * 20, "uint16"), ("t16", 16, bf), ("la16", 16, bf), ("lb16", 16, bf), ("lc16", 16, bf)]:
        SCRATCH[n] = ("sbuf", [128, w], t)
    for i in range(3):
        SCRATCH["sp%d" % i] = ("sbuf", [128, 3 * TW], "uint16")
        SCRATCH["sl%d" % i] = ("sbuf", [128, TW], "uint16")
        SCRATCH["lp%d" % i] = ("sbuf", [128, 3 * TW], "uint16")
        SCRATCH["la%d" % i] = ("sbuf", [128, TW], "uint16")
    SCRATCH["pa"] = ("psum", [128, 2048], f32)
    SCRATCH["pb"] = ("psum", [128, 2048], f32)


_decl()
LOADS = ["dfl", "dml", "dx", "du", "dv", "dwc", "dws"]
SEMAPHORES = ["cv", "cs_", "ct", "cg", "snt", "outs"] + LOADS + ["%s%d" % (n, i) for n in ("aq", "al", "aa") for i in range(3)]
TF = {n: i for i, n in enumerate(["jt", "f", "m", "hf", "fm", "cf", "hm", "cm", "ln", "cs", "pl", "g0", "g1", "g2", "g3", "i0", "ng", "t1", "p0", "pi", "u", "inv", "bq",
                                  "t2", "tp", "sw", "sg", "si", "sn", "e1", "wr", "wl", "pb", "kmd", "lx", "ple", "ple2", "c2", "pre0", "pre", "vv", "vp", "w", "l3"])}
TU = {n: i for i, n in enumerate(["tab%d" % k for k in range(9)] + ["m", "root", "l", "tp", "T", "sig", "b"] + ["end"])}
TI = {"k": 0, "root": 1, "d": 2, "n": 3}
BIAS = {"pp": 1.0, "lq": -2.0, "qz": 4.0, "tu.sig": 1.0}
H, HW = 192, 12
GAT, HALF, TINY, WAKE = 0.62, 0.32, 0.06, 0.15


def rank_program(g, core, T, topo):
    rank = T.rank_of(core)
    if rank is None:
        return
    A = AluOpType
    AF = ActivationFunctionType
    Q = {"v": g.vector, "s": g.scalar, "t": g.tensor, "g": g, "y": g.sync}
    CS = {"v": "cv", "s": "cs_", "t": "ct", "g": "cg"}
    prog = []

    def op(eng, fn, reads, writes, cost=TINY, sem=None, inc=1, lat=0.0, remote=None):
        prog.append({"eng": eng, "fn": fn, "r": reads, "w": writes, "c": cost, "sem": sem, "inc": inc, "lat": lat, "remote": remote})

    tf = lambda n: T.tf[:, TW * TF[n]:TW * TF[n] + TW]
    tu = lambda n, a=0, b=TW: T.tu[:, TW * TU[n] + a:TW * TU[n] + b]
    ti = lambda n: T.ti[:, TW * TI[n]:TW * TI[n] + TW]
    cl = lambda i: T.col[:, i:i + 1]
    SLOT = {"%s%d" % (n, k): (m, C * k) for n, m, z in (("ro", "ro", 9), ("c", "cc", 6)) for k in range(z)}

    def row(n):
        n, a = SLOT.get(n, (n, 0))
        return T[n][:, a:a + C]

    def sampled(n):
        n, a = SLOT.get(n, (n, 0))
        return T[n][:, a + 15:a + C:16]

    row1 = lambda n: T[n][:, 1:C + 1]
    win1 = lambda n: T[n][:, 0:C + 1]

    def tt(out, wk, a, b, o, rk, c=TINY):
        op("v", lambda: g.vector.tensor_tensor(out, a, b, o), rk, wk, c)

    def ts(out, wk, a, s1, s2, o0, o1, rk, c=TINY):
        if o1 is None:
            op("v", lambda: g.vector.tensor_scalar(out, a, s1, None, o0), rk, wk, c)
        else:
            op("v", lambda: g.vector.tensor_scalar(out, a, s1, s2, o0, o1), rk, wk, c)

    def cp(out, wk, a, rk, c=TINY):
        op("v", lambda: g.vector.tensor_copy(out, a), rk, wk, c)

    def act(out, wk, a, rk, c=GAT, func=None, **kw):
        op("s", lambda: g.scalar.activation(out, a, func or AF.Copy, **kw), rk, wk, c)

    def scan(out, wk, d0, d1, init, o0, o1, rk, c=0.43):
        op("v", lambda: g.vector.tensor_tensor_scan(out, d0, d1, init, o0, o1), rk, wk, c)

    def latch(ap, rk, cap, wk):
        scan(cap, [wk], ap, row("lc"), -1024.0, A.max, A.add, (rk if isinstance(rk, list) else [rk]) + ["lc"], 0.26)

    def tabs(cname, out, wk, col):
        ts(out, wk, sampled(cname), cl(col), None, A.add, None, [cname, "col%d" % col])

    def tabm(cname, out, wk, col):
        ts(out, wk, sampled(cname), -1.0, cl(col), A.mult, A.add, [cname, "col%d" % col])

    def load(eng, sem, out, src, key):
        op(eng, lambda: Q[eng].dma_start(out, src), [], [key], 0.07, sem=sem, inc=16, lat=2.0)
    load("y", "dfl", T.fl_s[:], T.fl[:], "fl_s")
    load("s", "dx", T.xin[:], T.x[:], "xin")
    load("y", "dml", T.ml_s[:], T.ml[:], "ml_s")
    load("y", "du", T.uin[:], T.u[:], "uin")
    load("y", "dwc", T.wq[:, 0:512].bitcast(dt.uint8), T.wc[:], "wq")
    load("y", "dws", T.wqs[:, 0:512], T.ws[:], "wqs")
    load("y", "dv", T.vin[:], T.v[:], "vin")

    def iota(out, wk, pattern, base, cm, n, flag=True):
        c = 0.15 + 0.00166 * n
        if flag:
            op("g", lambda: g.iota(out, pattern, base, cm, allow_small_or_imprecise_dtypes=True), [], wk, c)
        else:
            op("g", lambda: g.iota(out, pattern, base, cm), [], wk, c)
    iota(T.pq[:], ["pq"], [[0, TW]], 0, 1, TW, False)
    iota(T.t16[:], ["t16"], [[1, 16]], 0, 0, 16)
    iota(T.ramp[:], ["ramp"], [[1, C + 16]], -224, 0, C + 16)
    iota(row("k0"), ["k0"], [[1024, C]], 0, 0, C)
    iota(row("k0m"), ["k0m"], [[1024, C]], -1, 0, C)
    iota(tf("jt"), ["jt0"], [[16, TW]], 0, 0, TW)
    iota(T.ofi[:], ["ofi"], [[16, 8]], 0, 0, 8, False)
    iota(row("cpr"), ["cpr"], [[-1, C]], 449, 0, C)
    iota(row("kd"), ["kd"], [[1024, C]], -1536, 0, C)
    iota(row("kc"), ["kc"], [[1024, C]], -512, 0, C)
    ts(T.pqm[:], ["pqm"], T.pq[:], 15, None, A.bitwise_and, None, ["pq"])
    cp(cl(0), ["col0"], T.pqm[:, 0:1], ["pqm"])
    cp(T.ofq[:], ["ofq"], T.pqm[:], ["pqm"])
    ts(T.t16[:], ["t16"], T.t16[:], cl(0), None, A.subtract, None, ["t16", "col0"])
    ts(T.la16[:], ["la16"], T.t16[:], 0.0, -1024.0, A.is_lt, A.mult, ["t16"])
    ts(T.lb16[:], ["lb16"], T.t16[:], 0.0, 512.0, A.is_equal, A.mult, ["t16"])
    tt(T.la16[:], ["la16"], T.la16[:], T.lb16[:], A.add, ["la16", "lb16"])
    ts(T.lb16[:], ["lb16"], T.t16[:], 15.0, -1024.0, A.is_equal, A.mult, ["t16"])
    tt(T.lc16[:], ["lc16"], T.la16[:], T.lb16[:], A.add, ["la16", "lb16"])
    act(row("lc"), ["lc"], T.lc16[:].indirect(T.ofq[:]), ["lc16", "ofq"])
    act(row("lck"), ["lck"], row("lc"), ["lc"], 0.43, scale=1024.0)
    ts(cl(1), ["col1"], cl(0), 0.0, 1024.0, A.is_equal, A.mult, ["col0"])
    ts(cl(1), ["col1"], cl(1), -512.0, None, A.add, None, ["col1"])
    ts(cl(2), ["col2"], cl(1), 224.0, None, A.add, None, ["col1"])
    ts(cl(3), ["col3"], cl(1), 1024.0, 511.0, A.mult, A.add, ["col1"])
    ts(cl(8), ["col8"], cl(1), 1024.0, 512.0, A.mult, A.add, ["col1"])
    ts(cl(7), ["col7"], cl(1), -2.0, 1.0, A.mult, A.add, ["col1"])
    ts(cl(6), ["col6"], cl(1), 511.0 / 1024 + 0.01, None, A.add, None, ["col1"])
    ts(cl(4), ["col4"], cl(1), -1.0, 449.0, A.mult, A.add, ["col1"])
    ts(cl(5), ["col5"], cl(1), -1.0, 224.0, A.mult, A.add, ["col1"])
    for n in ["cp", "rst", "pm", "cm"]:
        op("v", lambda n=n: g.vector.memset(T[n][:, 0:1], 0.0), [], [n + "0"])
    op("v", lambda: g.vector.memset(T.ar[:, 0:1], 0.0), [], ["ar0"])
    op("v", lambda: g.vector.memset(T.et[:], 0.5), [], ["et1"], 0.5)
    op("g", lambda: g.affine_select(T.et[:], T.et[:], [[-1, 4], [1, 512]], A.is_equal, 0.0, 0, -4), ["et1"], ["et"], 3.6)
    cp(tu("tab0"), ["tu.tab0"], T.fl_s[:], ["fl_s"])

    KS, KM = ["ka", "kb"], ["kma", "kmb"]

    def frow():
        act(row("ro0"), ["ro0"], T.ramp[:].indirect(tu("tab0")), ["ramp", "tu.tab0"])

    def levels():
        for k in range(9):
            if k < 8:
                a, b = "ro%d" % k, "ro%d" % (k + 1)
                act(row(b), [b], row(a).indirect(tu("tab%d" % k)), [a, "tu.tab%d" % k])
            src = "k0" if k == 0 else KS[k % 2]
            sm = "k0m" if k == 0 else KM[k % 2]
            dst, dm = KS[(k + 1) % 2], KM[(k + 1) % 2]
            tt(row(dst), [dst], row(src).indirect(tu("tab%d" % k)), row(sm), A.min, [src, sm, "tu.tab%d" % k], GAT)
            if k < 8:
                c = "c%d" % (k % 2)
                latch(row(b), b, row(c), c)
                tabs(c, tu("tab%d" % (k + 1)), ["tu.tab%d" % (k + 1)], 2)
                act(row(dm), [dm], row(dst), [dst], 0.43, bias=-float(2 ** (k + 1)))

    KF = KS[1]

    def send(r, dst_name, src_name, rk, sem, code=False, w=C):
        dst = T.cores[rank ^ STEP[r]]
        rid, pid = topo.addr(dst)[0:2]
        m = topo.mask(core, dst)
        n = len(topo.engines(core, dst))
        if code:
            o, i = T[dst_name][:, 0:w].bitcast(dt.uint8), T[src_name][:, 0:w].bitcast(dt.uint8)
        else:
            o, i = T[dst_name][:, 0:w], T[src_name][:, 0:w]
        op("g", lambda: g.remote_dma(out_ap=o, in_ap=i, remote_sem=T.sem[sem], local_sem=T.sem.snt, pid=pid, routing_id=rid, dma_engine_mask=m),
           rk, [dst_name], 0.5, lat=4.0 + (6.0 if code else 0.0), remote=(sem, n))

    def finish(r):
        sp, sl = "sp%d" % r, "sl%d" % r
        tt(row("yk"), ["yk"], row(KF).indirect(tu("tab0")), row("kc"), A.max, [KF, "tu.tab0", "kc"], GAT)
        scan(row("ck"), ["ck"], row(KF), row("lck"), -1048576.0, A.max, A.add, [KF, "lck"])
        ts(tu("root"), ["tu.root"], T.ck[:, 15:C:16], 2.0 ** -10, cl(6), A.mult, A.add, ["ck", "col6"])
        ts(ti("k"), ["ti.k"], T.ck[:, 15:C:16], cl(3), None, A.add, None, ["ck", "col3"])
        ts(ti("d"), ["ti.d"], ti("k"), 511, None, A.bitwise_and, None, ["ti.k"])
        cp(T[sp][:, 2 * TW:3 * TW], [sp + "d"], ti("d"), ["ti.d"])
        tt(tf("kmd"), ["tf.kmd"], ti("k"), ti("d"), A.subtract, ["ti.k", "ti.d"])
        act(row("yr"), ["yr"], row("yk").indirect(tu("root")), ["yk", "tu.root"])
        act(row("drow"), ["drow"], T.ramp[:].indirect(T[sp][:, 2 * TW:3 * TW]), ["ramp", sp + "d"])
        scan(row("cs"), ["cs"], row("yk"), row("kd"), -1024.0 - 224.0 - 511.0, A.add, A.subtract, ["yk", "kd"])
        tt(row("plg"), ["plg"], row("cs").indirect(tu("root")), row(KF), A.subtract, ["cs", "tu.root", KF], GAT)
        latch(row("plg"), "plg", row("c2"), "c2")
        tabs("c2", T[sp][:, 0:TW], [sp + "a"], 2)
        op("v", lambda: g.vector.tensor_copy(win1("cp").indirect(T[sp][:, 0:TW]), row("cpr")), ["cpr", sp + "a", "cp0"], ["cp"], 1.4)
        scan(row("cl"), ["cl"], row("yr"), row("lck"), -1048576.0, A.max, A.add, ["yr", "lck"])
        ts(tf("lx"), ["tf.lx"], T["cl"][:, 15:C:16], cl(8), None, A.add, None, ["cl", "col8"])
        tt(tf("ln"), ["tf.ln"], tf("lx"), tf("kmd"), A.subtract, ["tf.lx", "tf.kmd"])
        cp(T[sp][:, TW:2 * TW], [sp + "b"], tf("ln"), ["tf.ln"])
        tabs("c2", tf("pl"), ["tf.pl"], 2)
        ts(tf("ple"), ["tf.ple"], tf("pl"), cl(2), None, A.subtract, None, ["tf.pl", "col2"])
        ts(tf("ple2"), ["tf.ple2"], tf("ple"), cl(2), None, A.subtract, None, ["tf.ple", "col2"])
        tt(tf("cs"), ["tf.cs"], tf("pl"), ti("d"), A.add, ["tf.pl", "ti.d"])
        cp(tu("end"), ["tu.end"], tf("cs"), ["tf.cs"])
        ts(tf("c2"), ["tf.c2"], tf("cf"), -2.0, None, A.mult, None, ["tf.cf"])
        ts(tf("pre0"), ["tf.pre0"], tf("cf"), cl(7), None, A.mult, None, ["tf.cf", "col7"])
        tt(tf("pre"), ["tf.pre"], tf("pre0"), tf("hf"), A.add, ["tf.pre0", "tf.hf"])
        send(r, "lp%d" % r, sp, [sp + "a", sp + "b", sp + "d"], "al%d" % r, w=3 * TW)
        latch(row1("cp"), "cp", row("c4"), "c4")
        tabm("c4", T[sl][:], [sl], 4)
        send(r, "la%d" % r, sl, [sl], "aa%d" % r, w=TW)

    def mm(dst, b, st, so, mv):
        op("t", lambda: g.tensor.matmul_mx(T[dst][:, 512 * b:512 * b + C], T[st][:, so:so + 128], T[st + "s"][:, so:so + 128], T[mv][:, 0:C], T[mv + "s"][:, 0:C], True, True),
           [st, st + "s", mv, mv + "s"], [dst + str(b)], 0.4)

    def quant(tile, keys, w, q):
        op("v", lambda: g.vector.quantize_mx(T[q][:, 0:w], T[q + "s"][:, 0:w], T[tile][:, 0:4 * w]), keys, [q, q + "s"], 0.08 + 0.00088 * w)

    def state_made(r):
        send(r, "lq%d" % r, "qx%d" % r, ["qx%d" % r], "aq%d" % r, code=True)
        send(r, "lq%ds" % r, "qx%ds" % r, ["qx%ds" % r], "aq%d" % r)
        mm("pb", 0, "qur", 0, "qx%d" % r)
        act(row("sr"), ["sr"], T.pb[:, 0:C], ["pb0", "ro8"], 0.43)
        for b in range(4):
            mm("pa", b, "qe", 128 * b, "qx%d" % r)
        for b in range(4):
            mm("pb", b, "qe", 128 * b, "lq%d" % r)

    frow()
    levels()
    cp(tu("m"), ["tu.m"], T.ml_s[:], ["ml_s"])
    cp(tf("f"), ["tf.f"], T.fl_s[:], ["fl_s"])
    cp(tf("m"), ["tf.m"], T.ml_s[:], ["ml_s"])
    act(row("fmr"), ["fmr"], row("ro0").indirect(tu("m")), ["ro0", "tu.m", "ro8"])
    latch(row("fmr"), "fmr", row("c2"), "c2")
    tabs("c2", tf("fm"), ["tf.fm"], 2)
    tt(tf("hf"), ["tf.hf"], tf("fm"), tf("f"), A.add, ["tf.fm", "tf.f"])
    ts(tf("hf"), ["tf.hf"], tf("hf"), 0.5, None, A.mult, None, ["tf.hf"])
    tt(tf("cf"), ["tf.cf"], tf("f"), tf("hf"), A.subtract, ["tf.f", "tf.hf"])
    ts(tf("jt"), ["tf.jt"], tf("jt"), cl(0), None, A.add, None, ["jt0", "col0"])
    tt(tf("hm"), ["tf.hm"], tf("m"), tf("jt"), A.add, ["tf.m", "tf.jt"])
    ts(tf("hm"), ["tf.hm"], tf("hm"), 0.5, None, A.mult, None, ["tf.hm"])
    tt(tf("cm"), ["tf.cm"], tf("jt"), tf("hm"), A.subtract, ["tf.jt", "tf.hm"])
    ts(tf("sn"), ["tf.sn"], tf("cm"), 0.0, 2.0, A.is_lt, A.mult, ["tf.cm"])
    ts(tu("sig"), ["tu.sig"], tf("sn"), 223.0, None, A.add, None, ["tf.sn"])
    act(row("sgn"), ["sgn"], T.ramp[:].indirect(tu("sig")), ["ramp", "tu.sig", "ro8"])
    quant("xin", ["xin", "tu.tab2"], C, "qx0")
    quant("uin", ["uin"], 128, "qu")
    cp(T.ofu[:], ["ofu"], T.ofi[:], ["ofi"])
    op("v", lambda: g.vector.tensor_copy(T.qur[:, 0:128].bitcast(dt.uint32), T.qu[:, 0:128].bitcast(dt.uint32).indirect(T.ofu[:, 0:8])), ["qu", "ofu"], ["qur"], 0.27)
    op("s", lambda: g.scalar.activation(T.qurs[:, 0:128], T.qus[:, 0:128].indirect(T.ofu[:, 0:8]), AF.Copy), ["qus", "ofu"], ["qurs"], 0.27)
    quant("et", ["et"], 512, "qe")
    state_made(0)
    finish(0)
    act(row("nsgn"), ["nsgn"], row("sgn"), ["sgn", "yr"], 0.43, scale=-1.0)
    ts(tf("e1"), ["tf.e1"], ti("d"), 1.0, None, A.add, None, ["ti.d"])
    tt(tf("wr"), ["tf.wr"], tf("e1"), tf("ln"), A.is_equal, ["tf.e1", "tf.ln"])
    tt(tf("wl"), ["tf.wl"], tf("wr"), tf("ln"), A.mult, ["tf.wr", "tf.ln"])
    tt(tf("pb"), ["tf.pb"], tf("pl"), tf("wl"), A.add, ["tf.pl", "tf.wl"])
    ts(tu("b"), ["tu.b"], tf("pb"), -1.0, None, A.add, None, ["tf.pb"])
    act(row("brow"), ["brow"], win1("cp").indirect(tu("b")), ["cp", "tu.b"], scale=-1.0, bias=225.0)
    latch(row("brow"), "brow", row("c3"), "c3")
    tabs("c3", tu("b"), ["tu.b"], 2)

    grs = lambda i: T.gr[:, C * i:C * i + C]
    for r in range(3):
        sl, lp, la, sp = "sl%d" % r, "lp%d" % r, "la%d" % r, "sp%d" % r
        last = r == 2
        act(row1("rst"), ["rst"], row("drow").indirect(T[sl][:]), ["drow", sl, "rst0"], scale=float(2 ** 90), bias=223.5 * float(2 ** 90))
        cp(row("sa"), ["sa"], row("sr").indirect(T[sl][:]), ["sr", sl], GAT)
        scan(row1("pm"), ["pm"], row("rst"), row("sa"), -float(2 ** 90), A.min, A.max, ["rst", "rst0", "sa", "pm0"])
        tt(row("eq"), ["eq"], win1("pm").indirect(tu("end")), row("sr"), A.is_equal, ["pm", "tu.end", "sr"], GAT)
        tt(row("cand"), ["cand"], row("eq").indirect(T[sl][:]), row1("cp"), A.mult, ["eq", sl, "cp"], GAT)
        scan(row1("cm"), ["cm"], row("rst"), row("cand"), 0.0, A.min, A.max, ["rst", "cand", "cm0"])
        act(T.lrow[:, 0:H], ["lrowa"], win1("cm").indirect(tu("end", 0, HW)), ["cm", "tu.end"], HALF, bias=-225.0)
        ts(T.lrow[:, H:C], ["lrowb"], win1("cm").indirect(tu("end", HW)), -225.0, None, A.add, None, ["cm", "tu.end"], HALF)
        latch(row("lrow"), ["lrowa", "lrowb"], row("c5"), "c5")
        tabm("c5", tu("l"), ["tu.l"], 5)
        act(row("plr"), ["plr"], T.ramp[:].indirect(T[sp][:, 0:TW]), ["ramp", sp + "a"])
        for b in range(4):
            act(row("fh%d" % b), ["fh%d" % b], T.pa[:, 512 * b:512 * b + C], ["pa%d" % b, "yr"], 0.43)
        act(row("tcsr"), ["tcsr"], T.ramp[:].indirect(T[lp][:, 2 * TW:3 * TW]), ["ramp", lp])
        act(row("tlenr"), ["tlenr"], T.ramp[:].indirect(T[lp][:, TW:2 * TW]), ["ramp", lp])
        act(row("tplr"), ["tplr"], T.ramp[:].indirect(T[lp][:, 0:TW]), ["ramp", lp])
        cp(grs(3), ["gr3"], row("tlenr").indirect(tu("l")), ["tlenr", "tu.l"], GAT)
        act(grs(1), ["gr1"], row("plr").indirect(tu("l")), ["plr", "tu.l"])
        cp(grs(2), ["gr2"], row("tcsr").indirect(tu("l")), ["tcsr", "tu.l"], GAT)
        act(grs(0), ["gr0"], row("tplr").indirect(tu("l")), ["tplr", "tu.l"])
        act(row1("ar"), ["ar"], T.ramp[:].indirect(T[la][:]), ["ramp", la, "ar0"])
        for i in (3, 1, 2, 0):
            latch(grs(i), "gr%d" % i, T.c4s[:, C * i:C * i + C], "c4s%d" % i)
        x = lambda i: T.c4s[:, C * i + 15:C * i + C:16]
        for b in range(4):
            act(row("ft%d" % b), ["ft%d" % b], T.pb[:, 512 * b:512 * b + C], ["pb%d" % b, "gr0"], 0.43)
        ts(tf("l3"), ["tf.l3"], x(3), cl(2), None, A.add, None, ["c4s3", "col2"])
        tt(tf("ng"), ["tf.ng"], tf("ple"), x(1), A.is_lt, ["c4s1", "tf.ple"])
        tt(tf("vv"), ["tf.vv"], tf("ple2"), x(1), A.subtract, ["c4s1", "tf.ple2"])
        tt(tf("vp"), ["tf.vp"], tf("pl"), x(1), A.subtract, ["c4s1", "tf.pl"])
        op("v", lambda: g.vector.reciprocal(tf("inv"), tf("l3")), ["tf.l3"], ["tf.inv"], 0.33)
        tt(tf("t1"), ["tf.t1"], tf("ng"), tf("ln"), A.mult, ["tf.ng", "tf.ln"])
        tt(tf("w"), ["tf.w"], x(2), tf("vv"), A.subtract, ["c4s2", "tf.vv"])
        tt(tf("u"), ["tf.u"], tf("w"), tf("t1"), A.subtract, ["tf.w", "tf.t1"])
        tt(tf("p0"), ["tf.p0"], x(0), tf("vp"), A.add, ["c4s0", "tf.vp"])
        tt(tf("pi"), ["tf.pi"], tf("p0"), tf("t1"), A.add, ["tf.p0", "tf.t1"])
        tt(tf("bq"), ["tf.bq"], tf("u"), tf("inv"), A.mult, ["tf.u", "tf.inv"])
        ts(ti("n"), ["ti.n"], tf("bq"), -0.4989, None, A.add, None, ["tf.bq"])
        tt(tf("t2"), ["tf.t2"], ti("n"), tf("l3"), A.mult, ["ti.n", "tf.l3"])
        tt(tf("tp"), ["tf.tp"], tf("pi"), tf("t2"), A.add, ["tf.pi", "tf.t2"])
        cp(tu("tp"), ["tu.tp"], tf("tp"), ["tf.tp"])
        act(T.trow[:, 0:H], ["trowa"], win1("ar").indirect(tu("tp", 0, HW)), ["ar", "tu.tp"], HALF)
        cp(T.trow[:, H:C], ["trowb"], win1("ar").indirect(tu("tp", HW)), ["ar", "tu.tp"], HALF)
        latch(row("trow"), ["trowa", "trowb"], row("c5"), "c5")
        tabs("c5", tu("T"), ["tu.T"], 2)
        tt(row("mu"), ["mu"], row("sr").indirect(tu("T")), row("sgn"), A.mult, ["sr", "tu.T", "sgn"], GAT)
        for b in range(4):
            act(row("fs%d" % b), ["fs%d" % b], row("ft%d" % b).indirect(tu("T")), ["ft%d" % b, "tu.T"])
        tt(row("nu"), ["nu"], row("sr").indirect(tu("T")), row("nsgn"), A.mult, ["sr", "tu.T", "nsgn"], GAT)
        tt(row("sw"), ["sw"], row("mu").indirect(tu("m")), row("nu"), A.is_lt, ["mu", "nu", "tu.m"], GAT)
        latch(row("sw"), "sw", row("c5"), "c5")
        ts(tf("sw"), ["tf.sw"], sampled("c5"), -2.0, cl(7), A.mult, A.add, ["c5", "col7"])
        tt(tf("si"), ["tf.si"], sampled("c5"), tf("c2"), A.mult, ["c5", "tf.c2"])
        tt(tf("f"), ["tf.f"], tf("si"), tf("pre"), A.add, ["tf.si", "tf.pre"])
        tt(tf("cf"), ["tf.cf"], tf("sw"), tf("cf"), A.mult, ["tf.sw", "tf.cf"])
        cp(tu("tab0"), ["tu.tab0"], tf("f"), ["tf.f"])
        for b in range(4):
            tt(T.zt[:, b:4 * C:4], ["zt%d" % b], row("fh%d" % b).indirect(tu("tab0")), row("fs%d" % b), A.add, ["fh%d" % b, "fs%d" % b, "tu.tab0"], GAT)
        quant("zt", ["zt0", "zt1", "zt2", "zt3"], C, "qz")
        for b in range(4):
            mm("pb", b, "wq", 128 * b, "qz")
        tt(tf("sg"), ["tf.sg"], tf("sw"), tf("cm"), A.mult, ["tf.sw", "tf.cm"])
        tt(tf("si"), ["tf.si"], tf("sg"), tf("hm"), A.add, ["tf.sg", "tf.hm"])
        cp(tu("sig"), ["tu.sig"], tf("si"), ["tf.si"])
        act(row("srow"), ["srow"], T.ramp[:].indirect(tu("sig")), ["ramp", "tu.sig"])
        act(row("brow"), ["brow"], row("srow").indirect(tu("b")), ["srow", "tu.b"])
        latch(row("brow"), "brow", row("c3"), "c3")
        tabs("c3", tu("b"), ["tu.b"], 2)
        for b in range(4):
            act(row("r2%d" % b), ["r2%d" % b], T.pb[:, 512 * b:512 * b + C], ["pb%d" % b], 0.43, scale=0.015625)
        for b in range(4):
            if b >= 4 - NP and not last:
                act(row("pp%d" % b), ["pp%d" % b], row("r2%d" % b).indirect(tu("b")), ["r2%d" % b, "tu.b"])
                tt(T.xt[:, b:4 * C:4], ["xt%d" % b], row("pp%d" % b), T.pa[:, 512 * b:512 * b + C], A.add, ["pp%d" % b, "pa%d" % b], 0.43)
                continue
            tt(T.xt[:, b:4 * C:4], ["xt%d" % b], row("r2%d" % b).indirect(tu("b")), row("fh%d" % b), A.add, ["r2%d" % b, "fh%d" % b, "tu.b"], GAT)
        quant("xt", ["xt0", "xt1", "xt2", "xt3"], C, "qx%d" % (r + 1))
        if last:
            break
        frow()
        levels()
        state_made(r + 1)
        if r == 0:
            quant("vin", ["vin"], 128, "qv")
        finish(r + 1)
    def store(eng, out, src, keys):
        op(eng, lambda: Q[eng].dma_start(out, src), keys, [], 0.07, sem="outs", inc=16, lat=2.0)
    act(row("nlr"), ["nlr"], T.ramp[:].indirect(tu("tab0")), ["ramp", "tu.tab0"], bias=224.0)
    store("y", T.nl[:], T.nlr[0:128:16, :], ["nlr"])
    mm("pb", 0, "qv", 0, "qx3")
    store("y", T.oc[:], T.qx3[:, 0:C].bitcast(dt.uint8), ["qx3"])
    act(row("ysb"), ["ysb"], T.pb[:, 0:C], ["pb0"], 0.43)
    for k in range(4):
        store("y", T.osc[4 * k:4 * k + 4, :], T.qx3s[32 * k:32 * k + 4, 0:C], ["qx3s"])
    store("s", T.y[:], row("ysb"), ["ysb"])

    n = len(prog)
    deps, kids = [set() for _ in range(n)], [[] for _ in range(n)]
    lw, rd = {}, {}
    for i, p in enumerate(prog):
        for k in p["r"]:
            if k in lw:
                deps[i].add(lw[k])
        for k in p["w"]:
            if k in lw:
                deps[i].add(lw[k])
            deps[i].update(rd.get(k, []))
        for k in p["r"]:
            rd.setdefault(k, []).append(i)
        for k in p["w"]:
            lw[k], rd[k] = i, []
        deps[i].discard(i)
        for d in deps[i]:
            kids[d].append(i)
    prio = [0.0] * n
    for i in range(n - 1, -1, -1):
        prio[i] = prog[i]["c"] + prog[i]["lat"] + max([prio[k] + WAKE for k in kids[i]] + [0.0])
    for i in range(n):
        prio[i] += BIAS.get(prog[i]["w"][0].rstrip("0123456789") if prog[i]["w"] else "", 0.0)
    done, left, tq, order = {}, [len(d) for d in deps], {e: 0.0 for e in Q}, []
    ready = {e: [] for e in Q}
    for i in range(n):
        if not left[i]:
            ready[prog[i]["eng"]].append((0.0, i))
    while len(order) < n:
        pick = None
        for e in Q:
            if not ready[e]:
                continue
            t0 = max(tq[e], min(a for a, i in ready[e]))
            a, i = max((x for x in ready[e] if x[0] <= t0 + 1e-9), key=lambda x: (prio[x[1]], -x[1]))
            if pick is None or t0 < pick[0]:
                pick = (t0, e, a, i)
        t0, e, a, i = pick
        ready[e].remove((a, i))
        order.append(i)
        tq[e] = t0 + prog[i]["c"]
        done[i] = tq[e] + prog[i]["lat"] + WAKE
        for k in kids[i]:
            left[k] -= 1
            if not left[k]:
                ready[prog[k]["eng"]].append((max(done[d] for d in deps[k]), k))

    cnt = {s: 0 for s in SEMAPHORES}
    known = {e: {} for e in Q}
    clock, lastw, readers = {}, {}, {}

    def need(eng, ds):
        best = {}
        for s, v in ds:
            best[s] = max(best.get(s, 0), v)
        own = CS.get(eng)
        for s in sorted(best, key=lambda x: (x == own, x)):
            if known[eng].get(s, 0) >= best[s]:
                continue
            Q[eng].wait_ge(T.sem[s], best[s])
            for x, y in clock[(s, best[s])].items():
                known[eng][x] = max(known[eng].get(x, 0), y)

    landed = {"aq%d" % i: 2 for i in range(3)}
    for i in order:
        p = prog[i]
        ds = []
        for k in p["r"]:
            if k in lastw:
                ds.append(lastw[k])
        if p["remote"]:
            need("g", ds)
            p["fn"]()
            sem, m = p["remote"]
            cnt["snt"] += m
            cnt[sem] += m
            me = (sem, m * landed.get(sem, 1))
            clock[me] = {sem: me[1]}
            lastw[p["w"][0]] = me
            continue
        for k in p["w"]:
            if k in lastw:
                ds.append(lastw[k])
            ds += readers.get(k, [])
        need(p["eng"], ds)
        s = p["sem"] or CS[p["eng"]]
        cnt[s] += p["inc"]
        p["fn"]().then_inc(T.sem[s], p["inc"])
        me = (s, cnt[s])
        clock[me] = dict(known[p["eng"]])
        clock[me][s] = cnt[s]
        for k in p["r"]:
            readers.setdefault(k, []).append(me)
        for k in p["w"]:
            lastw[k] = me
            readers[k] = []
    for s in SEMAPHORES:
        if cnt[s] and known["g"].get(s, 0) < cnt[s]:
            g.wait_ge(T.sem[s], cnt[s])
